import numpy as np
import ml_dtypes


def mxq(x, axis, fmt="e4m3"):
    dtype, down = {"e4m3": (ml_dtypes.float8_e4m3fn, 7), "e5m2": (ml_dtypes.float8_e5m2, 14)}[fmt]
    v = np.moveaxis(np.asarray(x, np.float32).astype(ml_dtypes.bfloat16).astype(np.float64), axis, -1)
    blocks = v.reshape(v.shape[:-1] + (-1, 32))
    amax = np.abs(blocks).max(-1, keepdims=True)
    byte = np.maximum(np.where(amax > 0, np.frexp(amax)[1] - 1 + 127, 0) - down, 1)
    scale = np.exp2(byte - 127.0)
    codes = (blocks / scale).astype(np.float32).astype(dtype).astype(np.float64)
    return np.moveaxis((codes * scale).reshape(v.shape), -1, axis)


WIDE = False


def mx_kscale(k):
    if not WIDE:
        return np.ones(k)
    levels = np.array([10, -10, 5, -5, 0])
    if k % 512:
        return np.exp2(np.random.permutation(np.resize(levels, k // 32))).repeat(32)
    a = np.empty((k // 512, 16))
    for p in range(k // 512):
        a[p, :8] = np.random.permutation(np.resize(levels, 8))
        for g in range(8):
            far = levels[np.abs(levels - a[p, g]) >= 10]
            a[p, g + 8] = far[np.random.randint(len(far))]
    return np.exp2(a.ravel()).repeat(32)


def f64(x):
    return np.asarray(x).astype(np.float64)


def striped(idx):
    return np.tile(idx.reshape(-1, 16).T, (8, 1)).astype(np.uint16)


def unstriped(offs):
    return offs[:16].T.reshape(-1).astype(np.int64)


K, T, H, N = 1024, 128, 1024, 256


def setup_inputs():
    n = np.random.standard_normal
    s = mx_kscale(K)[:, None]
    u = mx_kscale(H)
    idx = np.random.permutation(H)
    v = np.empty(H)
    v[idx] = u
    return {
        "xT": (n((K, T)) * s).astype(np.float32),
        "w1": (n((K, H)) / np.sqrt(K) / s * v).astype(np.float32),
        "w2": (n((H, N)) / np.sqrt(H) / u[:, None]).astype(np.float32),
        "offs": striped(idx),
    }


def reference(xT, w1, w2, offs):
    idx = unstriped(offs)
    h = mxq(f64(w1), 0, "e4m3").T @ mxq(f64(xT), 0, "e4m3")
    return mxq(f64(w2), 0, "e4m3").T @ mxq(h[idx], 0, "e4m3")

@@ -1,0 +1,220 @@
+import concourse.mybir as mybir
+from concourse.masks import make_identity
+from contextlib import ExitStack
+
+K, T, H, N = 1024, 128, 1024, 256
+FLOPS = 2 * K * H * T + 2 * H * N * T
+
+F32 = mybir.dt.float32
+BF16 = mybir.dt.bfloat16
+U32 = mybir.dt.uint32
+U16 = mybir.dt.uint16
+U8 = mybir.dt.uint8
+FP8X4 = mybir.dt.float8_e4m3fn_x4
+COPY = mybir.ActivationFunctionType.Copy
+MULT = mybir.AluOpType.mult
+ADD = mybir.AluOpType.add
+
+P = 128
+J = 4
+KP = P * J
+
+
+def tile_picked_shuffle_mlp_none_perm_l_kernel(tc, xT, w1, w2, offs, out):
+    nc = tc.nc
+    with ExitStack() as ctx:
+        keep = ctx.enter_context(tc.tile_pool(name="keep", bufs=1))
+        psum = ctx.enter_context(tc.psum_pool(name="psum", bufs=1))
+
+        def sb(shape, dtype, name):
+            return keep.tile(shape, dtype, name=name, align_bytes=64)
+
+        def ps(shape, name, tag):
+            return psum.tile(shape, F32, name=name, tag=tag)
+
+        offsets = keep.tile([P, H // 16], U16, name="offsets")
+        x_raw = sb([P, 2, J, T], F32, "x_raw")
+        raws = {}
+        for q, j0, j1, c0, c1 in ((0, 0, 4, 0, 1024), (1, 0, 2, 0, 1024), (1, 2, 4, 0, 512), (1, 2, 4, 512, 768), (1, 2, 4, 768, 1024)):
+            raw = sb([P, j1 - j0, c1 - c0], F32, "w1_raw_%d_%d_%d" % (q, j0, c0))
+            src = w1[q * KP : (q + 1) * KP, :].rearrange("(p j) c -> p j c", j=J)
+            nc.sync.dma_start(out=raw[:], in_=src[:, j0:j1, c0:c1])
+            raws[q, j0, c0] = raw
+            if len(raws) == 1:
+                nc.sync.dma_start(out=x_raw[:].rearrange("p q j t -> p q (j t)"), in_=xT.rearrange("(q p j) t -> p q (j t)", q=2, j=J))
+            if len(raws) == 2:
+                nc.sync.dma_start(offsets[:], offs)
+        w2_raw = []
+        for q in range(2):
+            raw = sb([P, J, N], F32, "w2_raw_%d" % q)
+            nc.sync.dma_start(out=raw[:], in_=w2[q * KP : (q + 1) * KP, :].rearrange("(p j) c -> p j c", j=J))
+            w2_raw.append(raw)
+
+        ident = sb([P, P], F32, "ident")
+        make_identity(nc, ident[:])
+
+        x_grp = sb([P, 2, T, J], BF16, "x_grp")
+        x_cod = sb([P, 2, T], U32, "x_cod")
+        x_scl = sb([P, 2, T], U8, "x_scl")
+
+        h32 = sb([P, H], F32, "h32")
+        h16 = sb([P, H], BF16, "h16")
+        width = {0: 256, 256: 256, 512: 256, 768: 128, 896: 128}
+        banks = {}
+        for b in sorted(width):
+            banks[b] = ps([P, width[b]], "h_%d" % b, "bank_%d" % b)
+
+        grps = [sb([P, H, J], BF16, "w1_grp_%d" % q) for q in range(2)]
+
+        def interleave(engine, q, j0, j1, c0, lo, hi):
+            dst = grps[q][:, lo:hi, j0:j1]
+            src = raws[q, j0, c0][:, :, lo - c0 : hi - c0]
+            if j1 - j0 == J:
+                dst = dst.rearrange("p (b i) j -> p b j i", i=4)
+                src = src.rearrange("p j (b i) -> p b j i", i=4)
+            else:
+                src = src.rearrange("p j c -> p c j")
+            if engine == "v":
+                nc.vector.tensor_copy(out=dst, in_=src)
+            else:
+                nc.scalar.copy(out=dst, in_=src)
+
+        def interleave_x(engine, q):
+            dst = x_grp[:, q].rearrange("p (b i) j -> p b j i", i=4)
+            src = x_raw[:, q].rearrange("p j (b i) -> p b j i", i=4)
+            if engine == "v":
+                nc.vector.tensor_copy(out=dst, in_=src)
+            else:
+                nc.scalar.copy(out=dst, in_=src)
+
+        def quantise_x():
+            nc.vector.quantize_mx(
+                out=x_cod[:].rearrange("p q t -> p (q t)").bitcast(FP8X4),
+                scales=x_scl[:].rearrange("p q t -> p (q t)"),
+                in_=x_grp[:].rearrange("p q t j -> p (q t j)"),
+            )
+
+        def quantise(q, lo, hi):
+            n = hi - lo
+            cod = sb([P, n], U32, "w1_cod_%d_%d" % (q, lo))
+            scl = sb([P, n], U8, "w1_scl_%d_%d" % (q, lo))
+            nc.vector.quantize_mx(out=cod[:].bitcast(FP8X4), scales=scl[:], in_=grps[q][:, lo:hi].rearrange("p c j -> p (c j)"))
+            for c in sorted(width):
+                if lo <= c and c < hi:
+                    a = c - lo
+                    nc.tensor.matmul_mx(
+                        out=banks[c][:],
+                        lhsT=x_cod[:, q, :].bitcast(FP8X4),
+                        lhsT_scale=x_scl[:, q, :],
+                        rhs=cod[:, a : a + width[c]].bitcast(FP8X4),
+                        rhs_scale=scl[:, a : a + width[c]],
+                        start=(q == 0),
+                        stop=(q == 1),
+                    )
+
+        def window32(b, engine="v"):
+            if engine == "v":
+                nc.vector.tensor_copy(out=h32[:, b : b + width[b]], in_=banks[b][:])
+            else:
+                nc.scalar.copy(out=h32[:, b : b + width[b]], in_=banks[b][:])
+
+        def window16(b):
+            nc.scalar.copy(out=h16[:, b : b + width[b]], in_=banks[b][:])
+
+        interleave("s", 0, 0, 4, 0, 344, 512)
+        interleave("v", 0, 0, 4, 0, 0, 344)
+        interleave_x("s", 1)
+        interleave("v", 0, 0, 4, 0, 512, 856)
+        interleave("s", 0, 0, 4, 0, 856, 1024)
+        interleave_x("v", 0)
+        quantise_x()
+        quantise(0, 0, 512)
+        quantise(0, 512, 1024)
+        interleave("s", 1, 0, 2, 0, 688, 1024)
+        interleave("v", 1, 0, 2, 0, 0, 688)
+        interleave("s", 1, 2, 4, 0, 344, 512)
+        interleave("v", 1, 2, 4, 0, 0, 256)
+        interleave("v", 1, 2, 4, 0, 256, 344)
+        quantise(1, 0, 256)
+        quantise(1, 256, 512)
+        interleave("s", 1, 2, 4, 512, 688, 768)
+        interleave("v", 1, 2, 4, 512, 512, 688)
+        window32(0, 's')
+        window16(0)
+        window32(256, 's')
+        window16(256)
+        quantise(1, 512, 768)
+        interleave("v", 1, 2, 4, 768, 768, 896)
+        interleave("v", 1, 2, 4, 768, 896, 1024)
+        quantise(1, 768, 896)
+        quantise(1, 896, 1024)
+        window32(512)
+        window16(512)
+        window32(768)
+        window16(896)
+        window32(896)
+        window16(768)
+
+        w2_grp = []
+        w2_cod = []
+        w2_scl = []
+        for q in range(2):
+            grp = sb([P, N, J], BF16, "w2_grp_%d" % q)
+            if q == 0:
+                nc.gpsimd.tensor_scalar(out=grp[:], in0=w2_raw[q][:].rearrange("p j c -> p c j"), scalar1=1.0, scalar2=0.0, op0=MULT, op1=ADD)
+            else:
+                nc.gpsimd.tensor_scalar(out=grp[:, 128:], in0=w2_raw[q][:, :, 128:].rearrange("p j c -> p c j"), scalar1=1.0, scalar2=0.0, op0=MULT, op1=ADD)
+            w2_grp.append(grp)
+            cod = sb([P, N], U32, "w2_cod_%d" % q)
+            scl = sb([P, N], U8, "w2_scl_%d" % q)
+            w2_cod.append(cod)
+            w2_scl.append(scl)
+
+        picked = []
+        for q in range(2):
+            g = sb([P, KP], BF16, "picked_%d" % q)
+            view = g[:].rearrange("t (u p e) -> t p u e", u=2, e=2)
+            nc.vector.tensor_copy(out=view[:, 0:64], in_=h32[:].indirect(offsets[:, 32 * q : 32 * q + 16]))
+            nc.scalar.activation(out=view[:, 64:128], in_=h16[:].indirect(offsets[:, 32 * q + 16 : 32 * q + 32]), func=COPY)
+            picked.append(g)
+
+        nc.vector.tensor_copy(out=w2_grp[1][:, 0:128].rearrange("p (b i) j -> p b j i", i=4), in_=w2_raw[1][:, :, 0:128].rearrange("p j (b i) -> p b j i", i=4))
+
+        hg_grp = []
+        hg_cod = []
+        hg_scl = []
+        for q in range(2):
+            turned = ps([P, 2, T], "turned_%d" % q, "turned_%d" % q)
+            words = picked[q][:].bitcast(F32)
+            for u in range(2):
+                nc.tensor.transpose(turned[:, u, :], words[:, 128 * u : 128 * (u + 1)], ident[:])
+            grp = sb([P, T * J], BF16, "hg_grp_%d" % q)
+            nc.scalar.copy(out=grp[:].bitcast(F32).rearrange("p (t u) -> p t u", u=2), in_=turned[:].rearrange("p u t -> p t u"))
+            hg_grp.append(grp)
+            cod = sb([P, T], U32, "hg_cod_%d" % q)
+            scl = sb([P, T], U8, "hg_scl_%d" % q)
+            hg_cod.append(cod)
+            hg_scl.append(scl)
+
+        for q in range(2):
+            nc.vector.quantize_mx(out=w2_cod[q][:].bitcast(FP8X4), scales=w2_scl[q][:], in_=w2_grp[q][:].rearrange("p c j -> p (c j)"))
+            nc.vector.quantize_mx(out=hg_cod[q][:].bitcast(FP8X4), scales=hg_scl[q][:], in_=hg_grp[q][:])
+
+        accs = [ps([P, T], "acc_%d" % m, "bank_%d" % (256 * m)) for m in range(2)]
+        for q in range(2):
+            for m in range(2):
+                nc.tensor.matmul_mx(
+                    out=accs[m][:],
+                    lhsT=w2_cod[q][:, 128 * m : 128 * (m + 1)].bitcast(FP8X4),
+                    lhsT_scale=w2_scl[q][:, 128 * m : 128 * (m + 1)],
+                    rhs=hg_cod[q][:].bitcast(FP8X4),
+                    rhs_scale=hg_scl[q][:],
+                    start=(q == 0),
+                    stop=(q == 1),
+                )
+        res0 = sb([P, T], F32, "res0")
+        res1 = sb([P, T], F32, "res1")
+        nc.vector.tensor_copy(out=res0[:], in_=accs[0][:])
+        nc.sync.dma_start(out=out[0:128, :], in_=res0[:])
+        nc.scalar.copy(out=res1[:], in_=accs[1][:])
+        nc.scalar.dma_start(out=out[128:256, :], in_=res1[:])

@@ -12,12 +12,11 @@ U16 = mybir.dt.uint16
 U8 = mybir.dt.uint8
 FP8X4 = mybir.dt.float8_e4m3fn_x4
 COPY = mybir.ActivationFunctionType.Copy
-MULT = mybir.AluOpType.mult
-ADD = mybir.AluOpType.add
 
 P = 128
 J = 4
 KP = P * J
+SPLIT = 288
 
 
 def tile_picked_shuffle_mlp_none_perm_l_kernel(tc, xT, w1, w2, offs, out):
@@ -57,7 +56,6 @@ def tile_picked_shuffle_mlp_none_perm_l_kernel(tc, xT, w1, w2, offs, out):
         x_cod = sb([P, 2, T], U32, "x_cod")
         x_scl = sb([P, 2, T], U8, "x_scl")
 
-        h32 = sb([P, H], F32, "h32")
         h16 = sb([P, H], BF16, "h16")
         width = {0: 256, 256: 256, 512: 256, 768: 128, 896: 128}
         banks = {}
@@ -112,73 +110,54 @@ def tile_picked_shuffle_mlp_none_perm_l_kernel(tc, xT, w1, w2, offs, out):
                         stop=(q == 1),
                     )
 
-        def window32(b, engine="v"):
+        def window(engine, b):
             if engine == "v":
-                nc.vector.tensor_copy(out=h32[:, b : b + width[b]], in_=banks[b][:])
+                nc.vector.tensor_copy(out=h16[:, b : b + width[b]], in_=banks[b][:])
             else:
-                nc.scalar.copy(out=h32[:, b : b + width[b]], in_=banks[b][:])
+                nc.scalar.copy(out=h16[:, b : b + width[b]], in_=banks[b][:])
 
-        def window16(b):
-            nc.scalar.copy(out=h16[:, b : b + width[b]], in_=banks[b][:])
-
-        interleave("s", 0, 0, 4, 0, 344, 512)
-        interleave("v", 0, 0, 4, 0, 0, 344)
+        interleave("s", 0, 0, 4, 0, 336, 512)
+        interleave("v", 0, 0, 4, 0, 0, 336)
+        interleave("s", 0, 0, 4, 0, 848, 1024)
+        interleave("v", 0, 0, 4, 0, 512, 848)
+        interleave_x("s", 0)
         interleave_x("s", 1)
-        interleave("v", 0, 0, 4, 0, 512, 856)
-        interleave("s", 0, 0, 4, 0, 856, 1024)
-        interleave_x("v", 0)
         quantise_x()
         quantise(0, 0, 512)
         quantise(0, 512, 1024)
-        interleave("s", 1, 0, 2, 0, 688, 1024)
-        interleave("v", 1, 0, 2, 0, 0, 688)
-        interleave("s", 1, 2, 4, 0, 344, 512)
+        interleave("s", 1, 0, 2, 0, 640, 1024)
+        interleave("v", 1, 0, 2, 0, 0, 640)
+        interleave("s", 1, 2, 4, 0, 256, 512)
         interleave("v", 1, 2, 4, 0, 0, 256)
-        interleave("v", 1, 2, 4, 0, 256, 344)
+        interleave("v", 1, 2, 4, 512, 512, 768)
         quantise(1, 0, 256)
-        quantise(1, 256, 512)
-        interleave("s", 1, 2, 4, 512, 688, 768)
-        interleave("v", 1, 2, 4, 512, 512, 688)
-        window32(0, 's')
-        window16(0)
-        window32(256, 's')
-        window16(256)
-        quantise(1, 512, 768)
+        interleave("s", 1, 2, 4, 768, 896, 1024)
         interleave("v", 1, 2, 4, 768, 768, 896)
-        interleave("v", 1, 2, 4, 768, 896, 1024)
+        quantise(1, 256, 512)
+        quantise(1, 512, 768)
         quantise(1, 768, 896)
         quantise(1, 896, 1024)
-        window32(512)
-        window16(512)
-        window32(768)
-        window16(896)
-        window32(896)
-        window16(768)
+        for b in sorted(width):
+            window("s", b)
 
-        w2_grp = []
-        w2_cod = []
-        w2_scl = []
-        for q in range(2):
-            grp = sb([P, N, J], BF16, "w2_grp_%d" % q)
-            if q == 0:
-                nc.gpsimd.tensor_scalar(out=grp[:], in0=w2_raw[q][:].rearrange("p j c -> p c j"), scalar1=1.0, scalar2=0.0, op0=MULT, op1=ADD)
-            else:
-                nc.gpsimd.tensor_scalar(out=grp[:, 128:], in0=w2_raw[q][:, :, 128:].rearrange("p j c -> p c j"), scalar1=1.0, scalar2=0.0, op0=MULT, op1=ADD)
-            w2_grp.append(grp)
-            cod = sb([P, N], U32, "w2_cod_%d" % q)
-            scl = sb([P, N], U8, "w2_scl_%d" % q)
-            w2_cod.append(cod)
-            w2_scl.append(scl)
+        def interleave_w2(dst, q):
+            nc.vector.tensor_copy(out=dst.rearrange("p (b i) j -> p b j i", i=4), in_=w2_raw[q][:].rearrange("p j (b i) -> p b j i", i=4))
+
+        w2_cod = [sb([P, N], U32, "w2_cod_%d" % q) for q in range(2)]
+        w2_scl = [sb([P, N], U8, "w2_scl_%d" % q) for q in range(2)]
+
+        def quantise_w2(src, q):
+            nc.vector.quantize_mx(out=w2_cod[q][:].bitcast(FP8X4), scales=w2_scl[q][:], in_=src.rearrange("p c j -> p (c j)"))
+
+        interleave_w2(grps[1][:, H - N :, :], 0)
+        quantise_w2(grps[1][:, H - N :, :], 0)
 
         picked = []
         for q in range(2):
-            g = sb([P, KP], BF16, "picked_%d" % q)
-            view = g[:].rearrange("t (u p e) -> t p u e", u=2, e=2)
-            nc.vector.tensor_copy(out=view[:, 0:64], in_=h32[:].indirect(offsets[:, 32 * q : 32 * q + 16]))
-            nc.scalar.activation(out=view[:, 64:128], in_=h16[:].indirect(offsets[:, 32 * q + 16 : 32 * q + 32]), func=COPY)
+            g = keep.tile([P, N * J], BF16, name="picked_%d" % q, tag="picked_%d" % q, align_bytes=64)
+            nc.vector.tensor_copy(out=g[:, 0:SPLIT], in_=h16[:].indirect(offsets[:, 32 * q : 32 * q + SPLIT // 16]))
+            nc.scalar.activation(out=g[:, SPLIT:KP], in_=h16[:].indirect(offsets[:, 32 * q + SPLIT // 16 : 32 * q + 32]), func=COPY)
             picked.append(g)
-
-        nc.vector.tensor_copy(out=w2_grp[1][:, 0:128].rearrange("p (b i) j -> p b j i", i=4), in_=w2_raw[1][:, :, 0:128].rearrange("p j (b i) -> p b j i", i=4))
 
         hg_grp = []
         hg_cod = []
@@ -187,7 +166,7 @@ def tile_picked_shuffle_mlp_none_perm_l_kernel(tc, xT, w1, w2, offs, out):
             turned = ps([P, 2, T], "turned_%d" % q, "turned_%d" % q)
             words = picked[q][:].bitcast(F32)
             for u in range(2):
-                nc.tensor.transpose(turned[:, u, :], words[:, 128 * u : 128 * (u + 1)], ident[:])
+                nc.tensor.transpose(turned[:, u, :], words[:, u : 256 : 2], ident[:])
             grp = sb([P, T * J], BF16, "hg_grp_%d" % q)
             nc.scalar.copy(out=grp[:].bitcast(F32).rearrange("p (t u) -> p t u", u=2), in_=turned[:].rearrange("p u t -> p t u"))
             hg_grp.append(grp)
@@ -196,9 +175,12 @@ def tile_picked_shuffle_mlp_none_perm_l_kernel(tc, xT, w1, w2, offs, out):
             hg_cod.append(cod)
             hg_scl.append(scl)
 
-        for q in range(2):
-            nc.vector.quantize_mx(out=w2_cod[q][:].bitcast(FP8X4), scales=w2_scl[q][:], in_=w2_grp[q][:].rearrange("p c j -> p (c j)"))
-            nc.vector.quantize_mx(out=hg_cod[q][:].bitcast(FP8X4), scales=hg_scl[q][:], in_=hg_grp[q][:])
+        w2_grp = keep.tile([P, N * J], BF16, name="w2_grp", tag="picked_0", align_bytes=64)
+        w2_view = w2_grp[:].rearrange("p (c j) -> p c j", j=J)
+        interleave_w2(w2_view, 1)
+        nc.vector.quantize_mx(out=hg_cod[0][:].bitcast(FP8X4), scales=hg_scl[0][:], in_=hg_grp[0][:])
+        quantise_w2(w2_view, 1)
+        nc.vector.quantize_mx(out=hg_cod[1][:].bitcast(FP8X4), scales=hg_scl[1][:], in_=hg_grp[1][:])
 
         accs = [ps([P, T], "acc_%d" % m, "bank_%d" % (256 * m)) for m in range(2)]
         for q in range(2):

@@ -16,7 +16,7 @@ COPY = mybir.ActivationFunctionType.Copy
 P = 128
 J = 4
 KP = P * J
-SPLIT = 288
+SPLIT = 224
 
 
 def tile_picked_shuffle_mlp_none_perm_l_kernel(tc, xT, w1, w2, offs, out):
@@ -34,11 +34,11 @@ def tile_picked_shuffle_mlp_none_perm_l_kernel(tc, xT, w1, w2, offs, out):
         offsets = keep.tile([P, H // 16], U16, name="offsets")
         x_raw = sb([P, 2, J, T], F32, "x_raw")
         raws = {}
+        w1_raw = [sb([P, J, H], F32, "w1_raw_%d" % q) for q in range(2)]
         for q, j0, j1, c0, c1 in ((0, 0, 4, 0, 1024), (1, 0, 2, 0, 1024), (1, 2, 4, 0, 512), (1, 2, 4, 512, 768), (1, 2, 4, 768, 1024)):
-            raw = sb([P, j1 - j0, c1 - c0], F32, "w1_raw_%d_%d_%d" % (q, j0, c0))
             src = w1[q * KP : (q + 1) * KP, :].rearrange("(p j) c -> p j c", j=J)
-            nc.sync.dma_start(out=raw[:], in_=src[:, j0:j1, c0:c1])
-            raws[q, j0, c0] = raw
+            nc.sync.dma_start(out=w1_raw[q][:, j0:j1, c0:c1], in_=src[:, j0:j1, c0:c1])
+            raws[q, j0, c0] = q
             if len(raws) == 1:
                 nc.sync.dma_start(out=x_raw[:].rearrange("p q j t -> p q (j t)"), in_=xT.rearrange("(q p j) t -> p q (j t)", q=2, j=J))
             if len(raws) == 2:
@@ -66,7 +66,7 @@ def tile_picked_shuffle_mlp_none_perm_l_kernel(tc, xT, w1, w2, offs, out):
 
         def interleave(engine, q, j0, j1, c0, lo, hi):
             dst = grps[q][:, lo:hi, j0:j1]
-            src = raws[q, j0, c0][:, :, lo - c0 : hi - c0]
+            src = w1_raw[q][:, j0:j1, lo:hi]
             if j1 - j0 == J:
                 dst = dst.rearrange("p (b i) j -> p b j i", i=4)
                 src = src.rearrange("p j (b i) -> p b j i", i=4)
@@ -125,16 +125,19 @@ def tile_picked_shuffle_mlp_none_perm_l_kernel(tc, xT, w1, w2, offs, out):
         quantise_x()
         quantise(0, 0, 512)
         quantise(0, 512, 1024)
-        interleave("s", 1, 0, 2, 0, 640, 1024)
-        interleave("v", 1, 0, 2, 0, 0, 640)
-        interleave("s", 1, 2, 4, 0, 256, 512)
-        interleave("v", 1, 2, 4, 0, 0, 256)
-        interleave("v", 1, 2, 4, 512, 512, 768)
+        interleave("v", 1, 0, 2, 0, 768, 1024)
+        interleave("s", 1, 0, 2, 0, 512, 768)
+        interleave("s", 1, 0, 4, 0, 320, 512)
+        interleave("v", 1, 0, 4, 0, 0, 256)
+        interleave("v", 1, 0, 4, 0, 256, 320)
         quantise(1, 0, 256)
-        interleave("s", 1, 2, 4, 768, 896, 1024)
-        interleave("v", 1, 2, 4, 768, 768, 896)
         quantise(1, 256, 512)
+        interleave("s", 1, 2, 4, 0, 672, 768)
+        interleave("v", 1, 2, 4, 0, 512, 672)
         quantise(1, 512, 768)
+        interleave("s", 1, 2, 4, 0, 928, 1024)
+        interleave("v", 1, 2, 4, 0, 768, 896)
+        interleave("v", 1, 2, 4, 0, 896, 928)
         quantise(1, 768, 896)
         quantise(1, 896, 1024)
         for b in sorted(width):

@@ -16,7 +16,7 @@ COPY = mybir.ActivationFunctionType.Copy
 P = 128
 J = 4
 KP = P * J
-SPLIT = 224
+SPLIT = 256
 
 
 def tile_picked_shuffle_mlp_none_perm_l_kernel(tc, xT, w1, w2, offs, out):
@@ -25,34 +25,46 @@ def tile_picked_shuffle_mlp_none_perm_l_kernel(tc, xT, w1, w2, offs, out):
         keep = ctx.enter_context(tc.tile_pool(name="keep", bufs=1))
         psum = ctx.enter_context(tc.psum_pool(name="psum", bufs=1))
 
-        def sb(shape, dtype, name):
-            return keep.tile(shape, dtype, name=name, align_bytes=64)
+        def sb(shape, dtype, name, tag=None):
+            return keep.tile(shape, dtype, name=name, tag=tag or name, align_bytes=64)
 
         def ps(shape, name, tag):
             return psum.tile(shape, F32, name=name, tag=tag)
 
+        def copy(engine, dst, src):
+            if engine == "v":
+                nc.vector.tensor_copy(out=dst, in_=src)
+            else:
+                nc.scalar.copy(out=dst, in_=src)
+
+        def load(w, name, q, j0, j1, c0, c1, into=None):
+            raw = into if into is not None else sb([P, J, w.shape[1]], F32, name)
+            src = w[q * KP : (q + 1) * KP, :].rearrange("(p j) c -> p j c", j=J)
+            nc.sync.dma_start(out=raw[:, j0:j1, c0:c1], in_=src[:, j0:j1, c0:c1])
+            return (raw, j0, j1, c0)
+
+        def load_x():
+            nc.sync.dma_start(out=x_raw[:].rearrange("p q j t -> p q (j t)"), in_=xT.rearrange("(q p j) t -> p q (j t)", q=2, j=J))
+
         offsets = keep.tile([P, H // 16], U16, name="offsets")
         x_raw = sb([P, 2, J, T], F32, "x_raw")
-        raws = {}
-        w1_raw = [sb([P, J, H], F32, "w1_raw_%d" % q) for q in range(2)]
-        for q, j0, j1, c0, c1 in ((0, 0, 4, 0, 1024), (1, 0, 2, 0, 1024), (1, 2, 4, 0, 512), (1, 2, 4, 512, 768), (1, 2, 4, 768, 1024)):
-            src = w1[q * KP : (q + 1) * KP, :].rearrange("(p j) c -> p j c", j=J)
-            nc.sync.dma_start(out=w1_raw[q][:, j0:j1, c0:c1], in_=src[:, j0:j1, c0:c1])
-            raws[q, j0, c0] = q
-            if len(raws) == 1:
-                nc.sync.dma_start(out=x_raw[:].rearrange("p q j t -> p q (j t)"), in_=xT.rearrange("(q p j) t -> p q (j t)", q=2, j=J))
-            if len(raws) == 2:
-                nc.sync.dma_start(offsets[:], offs)
-        w2_raw = []
-        for q in range(2):
-            raw = sb([P, J, N], F32, "w2_raw_%d" % q)
-            nc.sync.dma_start(out=raw[:], in_=w2[q * KP : (q + 1) * KP, :].rearrange("(p j) c -> p j c", j=J))
-            w2_raw.append(raw)
+        a0 = load(w1, "a0", 0, 0, 4, 0, 1024)
+        load_x()
+        lo2 = load(w1, "b", 1, 0, 2, 0, 1024)
+        nc.sync.dma_start(offsets[:], offs)
+        load(w1, "b", 1, 2, 4, 0, 512, lo2[0])
+        load(w1, "b", 1, 2, 4, 512, 768, lo2[0])
+        load(w1, "b", 1, 2, 4, 768, 1024, lo2[0])
+        c0 = load(w2, "c0", 0, 0, 4, 0, N)
+        c1 = load(w2, "c1", 1, 0, 4, 0, N)
+        hi2 = (lo2[0], 2, 4, 0)
+        all4 = (lo2[0], 0, 4, 0)
 
         ident = sb([P, P], F32, "ident")
         make_identity(nc, ident[:])
 
-        x_grp = sb([P, 2, T, J], BF16, "x_grp")
+        grps = [sb([P, H, J], BF16, "w1_grp_%d" % q) for q in range(2)]
+        x_grp = sb([P, 2 * T, J], BF16, "x_grp")[:]
         x_cod = sb([P, 2, T], U32, "x_cod")
         x_scl = sb([P, 2, T], U8, "x_scl")
 
@@ -62,35 +74,30 @@ def tile_picked_shuffle_mlp_none_perm_l_kernel(tc, xT, w1, w2, offs, out):
         for b in sorted(width):
             banks[b] = ps([P, width[b]], "h_%d" % b, "bank_%d" % b)
 
-        grps = [sb([P, H, J], BF16, "w1_grp_%d" % q) for q in range(2)]
-
-        def interleave(engine, q, j0, j1, c0, lo, hi):
-            dst = grps[q][:, lo:hi, j0:j1]
-            src = w1_raw[q][:, j0:j1, lo:hi]
+        def interleave(engine, grp, piece, lo, hi):
+            raw, j0, j1, c0 = piece
+            dst = grp[:, lo:hi, j0:j1]
+            src = raw[:, j0:j1, lo:hi]
             if j1 - j0 == J:
                 dst = dst.rearrange("p (b i) j -> p b j i", i=4)
                 src = src.rearrange("p j (b i) -> p b j i", i=4)
             else:
                 src = src.rearrange("p j c -> p c j")
-            if engine == "v":
-                nc.vector.tensor_copy(out=dst, in_=src)
-            else:
-                nc.scalar.copy(out=dst, in_=src)
+            copy(engine, dst, src)
 
         def interleave_x(engine, q):
-            dst = x_grp[:, q].rearrange("p (b i) j -> p b j i", i=4)
+            dst = x_grp[:, q * T : (q + 1) * T, :].rearrange("p (b i) j -> p b j i", i=4)
             src = x_raw[:, q].rearrange("p j (b i) -> p b j i", i=4)
-            if engine == "v":
-                nc.vector.tensor_copy(out=dst, in_=src)
-            else:
-                nc.scalar.copy(out=dst, in_=src)
+            copy(engine, dst, src)
 
         def quantise_x():
             nc.vector.quantize_mx(
                 out=x_cod[:].rearrange("p q t -> p (q t)").bitcast(FP8X4),
                 scales=x_scl[:].rearrange("p q t -> p (q t)"),
-                in_=x_grp[:].rearrange("p q t j -> p (q t j)"),
+                in_=x_grp.rearrange("p c j -> p (c j)"),
             )
+
+        made = {}
 
         def quantise(q, lo, hi):
             n = hi - lo
@@ -99,91 +106,120 @@ def tile_picked_shuffle_mlp_none_perm_l_kernel(tc, xT, w1, w2, offs, out):
             nc.vector.quantize_mx(out=cod[:].bitcast(FP8X4), scales=scl[:], in_=grps[q][:, lo:hi].rearrange("p c j -> p (c j)"))
             for c in sorted(width):
                 if lo <= c and c < hi:
-                    a = c - lo
-                    nc.tensor.matmul_mx(
-                        out=banks[c][:],
-                        lhsT=x_cod[:, q, :].bitcast(FP8X4),
-                        lhsT_scale=x_scl[:, q, :],
-                        rhs=cod[:, a : a + width[c]].bitcast(FP8X4),
-                        rhs_scale=scl[:, a : a + width[c]],
-                        start=(q == 0),
-                        stop=(q == 1),
-                    )
+                    made[q, c] = (cod, scl, c - lo)
+
+        def multiply(q, c):
+            cod, scl, a = made[q, c]
+            nc.tensor.matmul_mx(
+                out=banks[c][:],
+                lhsT=x_cod[:, q, :].bitcast(FP8X4),
+                lhsT_scale=x_scl[:, q, :],
+                rhs=cod[:, a : a + width[c]].bitcast(FP8X4),
+                rhs_scale=scl[:, a : a + width[c]],
+                start=(q == 0),
+                stop=(q == 1),
+            )
 
         def window(engine, b):
-            if engine == "v":
-                nc.vector.tensor_copy(out=h16[:, b : b + width[b]], in_=banks[b][:])
-            else:
-                nc.scalar.copy(out=h16[:, b : b + width[b]], in_=banks[b][:])
+            copy(engine, h16[:, b : b + width[b]], banks[b][:])
 
-        interleave("s", 0, 0, 4, 0, 336, 512)
-        interleave("v", 0, 0, 4, 0, 0, 336)
-        interleave("s", 0, 0, 4, 0, 848, 1024)
-        interleave("v", 0, 0, 4, 0, 512, 848)
+        w2_cod = {}
+        w2_scl = {}
+
+        def quantise_w2(grp, q, tag=None):
+            w2_cod[q] = sb([P, N], U32, "w2_cod_%d" % q, tag)
+            w2_scl[q] = sb([P, N], U8, "w2_scl_%d" % q)
+            nc.vector.quantize_mx(out=w2_cod[q][:].bitcast(FP8X4), scales=w2_scl[q][:], in_=grp.rearrange("p c j -> p (c j)"))
+
+        def quantise_w2h(grp, q, m):
+            if m == 0:
+                w2_cod[q] = sb([P, N], U32, "w2_cod_%d" % q)
+                w2_scl[q] = sb([P, N], U8, "w2_scl_%d" % q)
+            cols = slice(128 * m, 128 * (m + 1))
+            nc.vector.quantize_mx(out=w2_cod[q][:, cols].bitcast(FP8X4), scales=w2_scl[q][:, cols], in_=grp[:, cols, :].rearrange("p c j -> p (c j)"))
+
+        picked = {}
+
+        def gather(q):
+            g = sb([P, N * J], BF16, "picked_%d" % q)
+            nc.vector.tensor_copy(out=g[:, 0:SPLIT], in_=h16[:].indirect(offsets[:, 32 * q : 32 * q + SPLIT // 16]))
+            nc.scalar.activation(out=g[:, SPLIT:KP], in_=h16[:].indirect(offsets[:, 32 * q + SPLIT // 16 : 32 * q + 32]), func=COPY)
+            picked[q] = g
+
+        turned = {}
+        hg_grp = {}
+        hg_cod = {}
+        hg_scl = {}
+
+        def turn(q):
+            turned[q] = ps([P, 2, T], "turned_%d" % q, "turned_%d" % q)
+            words = picked[q][:].bitcast(F32)
+            for u in range(2):
+                nc.tensor.transpose(turned[q][:, u, :], words[:, u : 256 : 2], ident[:])
+
+        def lay(engine, q):
+            hg_grp[q] = sb([P, T * J], BF16, "hg_grp_%d" % q)
+            copy(engine, hg_grp[q][:].bitcast(F32).rearrange("p (t u) -> p t u", u=2), turned[q][:].rearrange("p u t -> p t u"))
+
+        def quantise_h(q):
+            hg_cod[q] = sb([P, T], U32, "hg_cod_%d" % q)
+            hg_scl[q] = sb([P, T], U8, "hg_scl_%d" % q)
+            nc.vector.quantize_mx(out=hg_cod[q][:].bitcast(FP8X4), scales=hg_scl[q][:], in_=hg_grp[q][:])
+
+        interleave("s", grps[0], a0, 336, 512)
+        interleave("v", grps[0], a0, 0, 336)
+        interleave("s", grps[0], a0, 848, 1024)
+        interleave("v", grps[0], a0, 512, 848)
         interleave_x("s", 0)
         interleave_x("s", 1)
         quantise_x()
         quantise(0, 0, 512)
+        multiply(0, 0)
+        multiply(0, 256)
         quantise(0, 512, 1024)
-        interleave("v", 1, 0, 2, 0, 768, 1024)
-        interleave("s", 1, 0, 2, 0, 512, 768)
-        interleave("s", 1, 0, 4, 0, 320, 512)
-        interleave("v", 1, 0, 4, 0, 0, 256)
-        interleave("v", 1, 0, 4, 0, 256, 320)
+        multiply(0, 512)
+        multiply(0, 768)
+        multiply(0, 896)
+        interleave("s", grps[1], lo2, 256, 640)
+        interleave("v", grps[1], lo2, 640, 1024)
+        interleave("s", grps[1], hi2, 304, 512)
+        interleave("v", grps[1], all4, 0, 256)
+        interleave("v", grps[1], hi2, 256, 304)
         quantise(1, 0, 256)
+        multiply(1, 0)
         quantise(1, 256, 512)
-        interleave("s", 1, 2, 4, 0, 672, 768)
-        interleave("v", 1, 2, 4, 0, 512, 672)
+        multiply(1, 256)
+        interleave("s", grps[1], hi2, 640, 768)
+        interleave("v", grps[1], hi2, 512, 640)
         quantise(1, 512, 768)
-        interleave("s", 1, 2, 4, 0, 928, 1024)
-        interleave("v", 1, 2, 4, 0, 768, 896)
-        interleave("v", 1, 2, 4, 0, 896, 928)
+        multiply(1, 512)
+        interleave("s", grps[1], hi2, 896, 1024)
+        interleave("v", grps[1], hi2, 768, 896)
         quantise(1, 768, 896)
+        multiply(1, 768)
         quantise(1, 896, 1024)
-        for b in sorted(width):
-            window("s", b)
-
-        def interleave_w2(dst, q):
-            nc.vector.tensor_copy(out=dst.rearrange("p (b i) j -> p b j i", i=4), in_=w2_raw[q][:].rearrange("p j (b i) -> p b j i", i=4))
-
-        w2_cod = [sb([P, N], U32, "w2_cod_%d" % q) for q in range(2)]
-        w2_scl = [sb([P, N], U8, "w2_scl_%d" % q) for q in range(2)]
-
-        def quantise_w2(src, q):
-            nc.vector.quantize_mx(out=w2_cod[q][:].bitcast(FP8X4), scales=w2_scl[q][:], in_=src.rearrange("p c j -> p (c j)"))
-
-        interleave_w2(grps[1][:, H - N :, :], 0)
-        quantise_w2(grps[1][:, H - N :, :], 0)
-
-        picked = []
-        for q in range(2):
-            g = keep.tile([P, N * J], BF16, name="picked_%d" % q, tag="picked_%d" % q, align_bytes=64)
-            nc.vector.tensor_copy(out=g[:, 0:SPLIT], in_=h16[:].indirect(offsets[:, 32 * q : 32 * q + SPLIT // 16]))
-            nc.scalar.activation(out=g[:, SPLIT:KP], in_=h16[:].indirect(offsets[:, 32 * q + SPLIT // 16 : 32 * q + 32]), func=COPY)
-            picked.append(g)
-
-        hg_grp = []
-        hg_cod = []
-        hg_scl = []
-        for q in range(2):
-            turned = ps([P, 2, T], "turned_%d" % q, "turned_%d" % q)
-            words = picked[q][:].bitcast(F32)
-            for u in range(2):
-                nc.tensor.transpose(turned[:, u, :], words[:, u : 256 : 2], ident[:])
-            grp = sb([P, T * J], BF16, "hg_grp_%d" % q)
-            nc.scalar.copy(out=grp[:].bitcast(F32).rearrange("p (t u) -> p t u", u=2), in_=turned[:].rearrange("p u t -> p t u"))
-            hg_grp.append(grp)
-            cod = sb([P, T], U32, "hg_cod_%d" % q)
-            scl = sb([P, T], U8, "hg_scl_%d" % q)
-            hg_cod.append(cod)
-            hg_scl.append(scl)
-
-        w2_grp = keep.tile([P, N * J], BF16, name="w2_grp", tag="picked_0", align_bytes=64)
-        w2_view = w2_grp[:].rearrange("p (c j) -> p c j", j=J)
-        interleave_w2(w2_view, 1)
-        nc.vector.quantize_mx(out=hg_cod[0][:].bitcast(FP8X4), scales=hg_scl[0][:], in_=hg_grp[0][:])
-        quantise_w2(w2_view, 1)
-        nc.vector.quantize_mx(out=hg_cod[1][:].bitcast(FP8X4), scales=hg_scl[1][:], in_=hg_grp[1][:])
+        multiply(1, 896)
+        window("s", 0)
+        window("s", 256)
+        window("s", 512)
+        window("s", 768)
+        window("s", 896)
+        w2_first = grps[1][:, H - N :, :]
+        interleave("v", w2_first, c0, 0, 128)
+        interleave("v", w2_first, c0, 128, N)
+        quantise_w2h(w2_first, 0, 0)
+        quantise_w2h(w2_first, 0, 1)
+        gather(0)
+        gather(1)
+        turn(0)
+        lay("s", 0)
+        turn(1)
+        lay("s", 1)
+        w2_tile = sb([P, N, J], BF16, "w2_grp", "picked_0")
+        interleave("v", w2_tile[:], c1, 0, N)
+        quantise_h(0)
+        quantise_w2(w2_tile[:], 1)
+        quantise_h(1)
 
         accs = [ps([P, T], "acc_%d" % m, "bank_%d" % (256 * m)) for m in range(2)]
         for q in range(2):

@@ -233,9 +233,7 @@ def tile_picked_shuffle_mlp_none_perm_l_kernel(tc, xT, w1, w2, offs, out):
                     start=(q == 0),
                     stop=(q == 1),
                 )
-        res0 = sb([P, T], F32, "res0")
-        res1 = sb([P, T], F32, "res1")
-        nc.vector.tensor_copy(out=res0[:], in_=accs[0][:])
-        nc.sync.dma_start(out=out[0:128, :], in_=res0[:])
-        nc.scalar.copy(out=res1[:], in_=accs[1][:])
-        nc.scalar.dma_start(out=out[128:256, :], in_=res1[:])
+        res = sb([P, 2, T], F32, "res")
+        nc.vector.tensor_copy(out=res[:, 0, :], in_=accs[0][:])
+        nc.scalar.copy(out=res[:, 1, :], in_=accs[1][:])
+        nc.sync.dma_start(out=out.rearrange("(m p) t -> p m t", m=2), in_=res[:])

@@ -205,8 +205,11 @@ def tile_picked_shuffle_mlp_none_perm_l_kernel(tc, xT, w1, w2, offs, out):
         window("s", 768)
         window("s", 896)
         w2_first = grps[1][:, H - N :, :]
-        interleave("v", w2_first, c0, 0, 128)
-        interleave("v", w2_first, c0, 128, N)
+        for m in range(2):
+            nc.vector.tensor_copy(
+                out=w2_first[:, 128 * m : 128 * (m + 1), :].rearrange("p (b i) j -> p b j i", i=4),
+                in_=c0[0][:].rearrange("p j (b i m) -> p m b j i", i=4, m=2)[:, m],
+            )
         quantise_w2h(w2_first, 0, 0)
         quantise_w2h(w2_first, 0, 1)
         gather(0)
@@ -216,7 +219,10 @@ def tile_picked_shuffle_mlp_none_perm_l_kernel(tc, xT, w1, w2, offs, out):
         turn(1)
         lay("s", 1)
         w2_tile = sb([P, N, J], BF16, "w2_grp", "picked_0")
-        interleave("v", w2_tile[:], c1, 0, N)
+        nc.vector.tensor_copy(
+            out=w2_tile[:].rearrange("p (m b i) j -> p m b j i", i=4, m=2),
+            in_=c1[0][:].rearrange("p j (b i m) -> p m b j i", i=4, m=2),
+        )
         quantise_h(0)
         quantise_w2(w2_tile[:], 1)
         quantise_h(1)
@@ -236,4 +242,4 @@ def tile_picked_shuffle_mlp_none_perm_l_kernel(tc, xT, w1, w2, offs, out):
         res = sb([P, 2, T], F32, "res")
         nc.vector.tensor_copy(out=res[:, 0, :], in_=accs[0][:])
         nc.scalar.copy(out=res[:, 1, :], in_=accs[1][:])
-        nc.sync.dma_start(out=out.rearrange("(m p) t -> p m t", m=2), in_=res[:])
+        nc.sync.dma_start(out=out.rearrange("(p m) t -> p (m t)", m=2), in_=res[:].rearrange("p m t -> p (m t)"))

@@ -51,11 +51,11 @@ def tile_picked_shuffle_mlp_none_perm_l_kernel(tc, xT, w1, w2, offs, out):
         a0 = load(w1, "a0", 0, 0, 4, 0, 1024)
         load_x()
         lo2 = load(w1, "b", 1, 0, 2, 0, 1024)
-        nc.sync.dma_start(offsets[:], offs)
         load(w1, "b", 1, 2, 4, 0, 512, lo2[0])
         load(w1, "b", 1, 2, 4, 512, 768, lo2[0])
         load(w1, "b", 1, 2, 4, 768, 1024, lo2[0])
         c0 = load(w2, "c0", 0, 0, 4, 0, N)
+        nc.sync.dma_start(offsets[:], offs)
         c1 = load(w2, "c1", 1, 0, 4, 0, N)
         hi2 = (lo2[0], 2, 4, 0)
         all4 = (lo2[0], 0, 4, 0)
@@ -68,7 +68,7 @@ def tile_picked_shuffle_mlp_none_perm_l_kernel(tc, xT, w1, w2, offs, out):
         x_cod = sb([P, 2, T], U32, "x_cod")
         x_scl = sb([P, 2, T], U8, "x_scl")
 
-        h16 = sb([P, H], BF16, "h16")
+        h16 = sb([P, H], BF16, "h16", "window")
         width = {0: 256, 256: 256, 512: 256, 768: 128, 896: 128}
         banks = {}
         for b in sorted(width):
@@ -126,11 +126,6 @@ def tile_picked_shuffle_mlp_none_perm_l_kernel(tc, xT, w1, w2, offs, out):
         w2_cod = {}
         w2_scl = {}
 
-        def quantise_w2(grp, q, tag=None):
-            w2_cod[q] = sb([P, N], U32, "w2_cod_%d" % q, tag)
-            w2_scl[q] = sb([P, N], U8, "w2_scl_%d" % q)
-            nc.vector.quantize_mx(out=w2_cod[q][:].bitcast(FP8X4), scales=w2_scl[q][:], in_=grp.rearrange("p c j -> p (c j)"))
-
         def quantise_w2h(grp, q, m):
             if m == 0:
                 w2_cod[q] = sb([P, N], U32, "w2_cod_%d" % q)
@@ -141,14 +136,13 @@ def tile_picked_shuffle_mlp_none_perm_l_kernel(tc, xT, w1, w2, offs, out):
         picked = {}
 
         def gather(q):
-            g = sb([P, N * J], BF16, "picked_%d" % q)
+            g = sb([P, KP], BF16, "picked_%d" % q)
             nc.vector.tensor_copy(out=g[:, 0:SPLIT], in_=h16[:].indirect(offsets[:, 32 * q : 32 * q + SPLIT // 16]))
             nc.scalar.activation(out=g[:, SPLIT:KP], in_=h16[:].indirect(offsets[:, 32 * q + SPLIT // 16 : 32 * q + 32]), func=COPY)
             picked[q] = g
 
         turned = {}
         hg_grp = {}
-        hg_cod = {}
         hg_scl = {}
 
         def turn(q):
@@ -162,9 +156,8 @@ def tile_picked_shuffle_mlp_none_perm_l_kernel(tc, xT, w1, w2, offs, out):
             copy(engine, hg_grp[q][:].bitcast(F32).rearrange("p (t u) -> p t u", u=2), turned[q][:].rearrange("p u t -> p t u"))
 
         def quantise_h(q):
-            hg_cod[q] = sb([P, T], U32, "hg_cod_%d" % q)
             hg_scl[q] = sb([P, T], U8, "hg_scl_%d" % q)
-            nc.vector.quantize_mx(out=hg_cod[q][:].bitcast(FP8X4), scales=hg_scl[q][:], in_=hg_grp[q][:])
+            nc.vector.quantize_mx(out=hg_cod[:, q, :].bitcast(FP8X4), scales=hg_scl[q][:], in_=hg_grp[q][:])
 
         interleave("s", grps[0], a0, 336, 512)
         interleave("v", grps[0], a0, 0, 336)
@@ -185,16 +178,16 @@ def tile_picked_shuffle_mlp_none_perm_l_kernel(tc, xT, w1, w2, offs, out):
         interleave("s", grps[1], hi2, 304, 512)
         interleave("v", grps[1], all4, 0, 256)
         interleave("v", grps[1], hi2, 256, 304)
+        interleave("s", grps[1], hi2, 640, 768)
+        interleave("v", grps[1], hi2, 512, 640)
         quantise(1, 0, 256)
         multiply(1, 0)
         quantise(1, 256, 512)
         multiply(1, 256)
-        interleave("s", grps[1], hi2, 640, 768)
-        interleave("v", grps[1], hi2, 512, 640)
-        quantise(1, 512, 768)
-        multiply(1, 512)
         interleave("s", grps[1], hi2, 896, 1024)
         interleave("v", grps[1], hi2, 768, 896)
+        quantise(1, 512, 768)
+        multiply(1, 512)
         quantise(1, 768, 896)
         multiply(1, 768)
         quantise(1, 896, 1024)
@@ -218,13 +211,16 @@ def tile_picked_shuffle_mlp_none_perm_l_kernel(tc, xT, w1, w2, offs, out):
         lay("s", 0)
         turn(1)
         lay("s", 1)
-        w2_tile = sb([P, N, J], BF16, "w2_grp", "picked_0")
-        nc.vector.tensor_copy(
-            out=w2_tile[:].rearrange("p (m b i) j -> p m b j i", i=4, m=2),
-            in_=c1[0][:].rearrange("p j (b i m) -> p m b j i", i=4, m=2),
-        )
+        w2_tile = sb([P, N, J], BF16, "w2_grp", "window")
+        for m in range(2):
+            nc.vector.tensor_copy(
+                out=w2_tile[:, 128 * m : 128 * (m + 1), :].rearrange("p (b i) j -> p b j i", i=4),
+                in_=c1[0][:].rearrange("p j (b i m) -> p m b j i", i=4, m=2)[:, m],
+            )
+        hg_cod = sb([P, 2, T], U32, "hg_cod", "c1")
+        quantise_w2h(w2_tile[:], 1, 0)
         quantise_h(0)
-        quantise_w2(w2_tile[:], 1)
+        quantise_w2h(w2_tile[:], 1, 1)
         quantise_h(1)
 
         accs = [ps([P, T], "acc_%d" % m, "bank_%d" % (256 * m)) for m in range(2)]
@@ -234,7 +230,7 @@ def tile_picked_shuffle_mlp_none_perm_l_kernel(tc, xT, w1, w2, offs, out):
                     out=accs[m][:],
                     lhsT=w2_cod[q][:, 128 * m : 128 * (m + 1)].bitcast(FP8X4),
                     lhsT_scale=w2_scl[q][:, 128 * m : 128 * (m + 1)],
-                    rhs=hg_cod[q][:].bitcast(FP8X4),
+                    rhs=hg_cod[:, q, :].bitcast(FP8X4),
                     rhs_scale=hg_scl[q][:],
                     start=(q == 0),
                     stop=(q == 1),

@@ -26,7 +26,7 @@ def tile_picked_shuffle_mlp_none_perm_l_kernel(tc, xT, w1, w2, offs, out):
         psum = ctx.enter_context(tc.psum_pool(name="psum", bufs=1))
 
         def sb(shape, dtype, name, tag=None):
-            return keep.tile(shape, dtype, name=name, tag=tag or name, align_bytes=64)
+            return keep.tile(shape, dtype, name=name, tag=tag or name, align_bytes=256)
 
         def ps(shape, name, tag):
             return psum.tile(shape, F32, name=name, tag=tag)

@@ -69,7 +69,7 @@ def tile_picked_shuffle_mlp_none_perm_l_kernel(tc, xT, w1, w2, offs, out):
         x_scl = sb([P, 2, T], U8, "x_scl")
 
         h16 = sb([P, H], BF16, "h16", "window")
-        width = {0: 256, 256: 256, 512: 256, 768: 128, 896: 128}
+        width = {0: 256, 256: 256, 512: 128, 640: 128, 768: 128, 896: 128}
         banks = {}
         for b in sorted(width):
             banks[b] = ps([P, width[b]], "h_%d" % b, "bank_%d" % b)
@@ -171,6 +171,7 @@ def tile_picked_shuffle_mlp_none_perm_l_kernel(tc, xT, w1, w2, offs, out):
         multiply(0, 256)
         quantise(0, 512, 1024)
         multiply(0, 512)
+        multiply(0, 640)
         multiply(0, 768)
         multiply(0, 896)
         interleave("s", grps[1], lo2, 256, 640)
@@ -178,23 +179,26 @@ def tile_picked_shuffle_mlp_none_perm_l_kernel(tc, xT, w1, w2, offs, out):
         interleave("s", grps[1], hi2, 304, 512)
         interleave("v", grps[1], all4, 0, 256)
         interleave("v", grps[1], hi2, 256, 304)
-        interleave("s", grps[1], hi2, 640, 768)
-        interleave("v", grps[1], hi2, 512, 640)
+        interleave("s", grps[1], hi2, 592, 768)
+        interleave("v", grps[1], hi2, 512, 592)
         quantise(1, 0, 256)
         multiply(1, 0)
         quantise(1, 256, 512)
         multiply(1, 256)
         interleave("s", grps[1], hi2, 896, 1024)
         interleave("v", grps[1], hi2, 768, 896)
-        quantise(1, 512, 768)
+        quantise(1, 512, 640)
         multiply(1, 512)
+        quantise(1, 640, 768)
+        multiply(1, 640)
         quantise(1, 768, 896)
         multiply(1, 768)
         quantise(1, 896, 1024)
         multiply(1, 896)
-        window("s", 0)
+        window("v", 0)
         window("s", 256)
         window("s", 512)
+        window("s", 640)
         window("s", 768)
         window("s", 896)
         w2_first = grps[1][:, H - N :, :]
@@ -203,10 +207,10 @@ def tile_picked_shuffle_mlp_none_perm_l_kernel(tc, xT, w1, w2, offs, out):
                 out=w2_first[:, 128 * m : 128 * (m + 1), :].rearrange("p (b i) j -> p b j i", i=4),
                 in_=c0[0][:].rearrange("p j (b i m) -> p m b j i", i=4, m=2)[:, m],
             )
-        quantise_w2h(w2_first, 0, 0)
-        quantise_w2h(w2_first, 0, 1)
         gather(0)
         gather(1)
+        quantise_w2h(w2_first, 0, 0)
+        quantise_w2h(w2_first, 0, 1)
         turn(0)
         lay("s", 0)
         turn(1)

@@ -90,11 +90,11 @@ def tile_picked_shuffle_mlp_none_perm_l_kernel(tc, xT, w1, w2, offs, out):
             src = x_raw[:, q].rearrange("p j (b i) -> p b j i", i=4)
             copy(engine, dst, src)
 
-        def quantise_x():
+        def quantise_x(q):
             nc.vector.quantize_mx(
-                out=x_cod[:].rearrange("p q t -> p (q t)").bitcast(FP8X4),
-                scales=x_scl[:].rearrange("p q t -> p (q t)"),
-                in_=x_grp.rearrange("p c j -> p (c j)"),
+                out=x_cod[:, q, :].bitcast(FP8X4),
+                scales=x_scl[:, q, :],
+                in_=x_grp[:, q * T : (q + 1) * T, :].rearrange("p c j -> p (c j)"),
             )
 
         made = {}
@@ -159,25 +159,27 @@ def tile_picked_shuffle_mlp_none_perm_l_kernel(tc, xT, w1, w2, offs, out):
             hg_scl[q] = sb([P, T], U8, "hg_scl_%d" % q)
             nc.vector.quantize_mx(out=hg_cod[:, q, :].bitcast(FP8X4), scales=hg_scl[q][:], in_=hg_grp[q][:])
 
-        interleave("s", grps[0], a0, 336, 512)
-        interleave("v", grps[0], a0, 0, 336)
-        interleave("s", grps[0], a0, 848, 1024)
-        interleave("v", grps[0], a0, 512, 848)
+        interleave("s", grps[0], a0, 320, 512)
+        interleave("v", grps[0], a0, 0, 320)
+        interleave("s", grps[0], a0, 832, 1024)
+        interleave("v", grps[0], a0, 512, 832)
         interleave_x("s", 0)
-        interleave_x("s", 1)
-        quantise_x()
+        interleave_x("v", 1)
         quantise(0, 0, 512)
+        quantise_x(1)
+        quantise(0, 512, 1024)
+        interleave("s", grps[1], lo2, 128, 496)
+        interleave("v", grps[1], lo2, 496, 1024)
+        quantise_x(0)
         multiply(0, 0)
         multiply(0, 256)
-        quantise(0, 512, 1024)
         multiply(0, 512)
         multiply(0, 640)
         multiply(0, 768)
         multiply(0, 896)
-        interleave("s", grps[1], lo2, 256, 640)
-        interleave("v", grps[1], lo2, 640, 1024)
         interleave("s", grps[1], hi2, 304, 512)
-        interleave("v", grps[1], all4, 0, 256)
+        interleave("v", grps[1], all4, 0, 128)
+        interleave("v", grps[1], hi2, 128, 256)
         interleave("v", grps[1], hi2, 256, 304)
         interleave("s", grps[1], hi2, 592, 768)
         interleave("v", grps[1], hi2, 512, 592)

@@ -16,7 +16,7 @@ COPY = mybir.ActivationFunctionType.Copy
 P = 128
 J = 4
 KP = P * J
-SPLIT = 256
+SPLIT = (256, 256)
 
 
 def tile_picked_shuffle_mlp_none_perm_l_kernel(tc, xT, w1, w2, offs, out):
@@ -68,7 +68,7 @@ def tile_picked_shuffle_mlp_none_perm_l_kernel(tc, xT, w1, w2, offs, out):
         x_cod = sb([P, 2, T], U32, "x_cod")
         x_scl = sb([P, 2, T], U8, "x_scl")
 
-        h16 = sb([P, H], BF16, "h16", "window")
+        h16 = sb([P, H], BF16, "h16")
         width = {0: 256, 256: 256, 512: 128, 640: 128, 768: 128, 896: 128}
         banks = {}
         for b in sorted(width):
@@ -137,8 +137,9 @@ def tile_picked_shuffle_mlp_none_perm_l_kernel(tc, xT, w1, w2, offs, out):
 
         def gather(q):
             g = sb([P, KP], BF16, "picked_%d" % q)
-            nc.vector.tensor_copy(out=g[:, 0:SPLIT], in_=h16[:].indirect(offsets[:, 32 * q : 32 * q + SPLIT // 16]))
-            nc.scalar.activation(out=g[:, SPLIT:KP], in_=h16[:].indirect(offsets[:, 32 * q + SPLIT // 16 : 32 * q + 32]), func=COPY)
+            s = SPLIT[q]
+            nc.vector.tensor_copy(out=g[:, 0:s], in_=h16[:].indirect(offsets[:, 32 * q : 32 * q + s // 16]))
+            nc.scalar.activation(out=g[:, s:KP], in_=h16[:].indirect(offsets[:, 32 * q + s // 16 : 32 * q + 32]), func=COPY)
             picked[q] = g
 
         turned = {}
@@ -181,8 +182,8 @@ def tile_picked_shuffle_mlp_none_perm_l_kernel(tc, xT, w1, w2, offs, out):
         interleave("v", grps[1], all4, 0, 128)
         interleave("v", grps[1], hi2, 128, 256)
         interleave("v", grps[1], hi2, 256, 304)
-        interleave("s", grps[1], hi2, 592, 768)
-        interleave("v", grps[1], hi2, 512, 592)
+        interleave("s", grps[1], hi2, 560, 768)
+        interleave("v", grps[1], hi2, 512, 560)
         quantise(1, 0, 256)
         multiply(1, 0)
         quantise(1, 256, 512)
@@ -197,9 +198,9 @@ def tile_picked_shuffle_mlp_none_perm_l_kernel(tc, xT, w1, w2, offs, out):
         multiply(1, 768)
         quantise(1, 896, 1024)
         multiply(1, 896)
-        window("v", 0)
+        window("s", 0)
         window("s", 256)
-        window("s", 512)
+        window("v", 512)
         window("s", 640)
         window("s", 768)
         window("s", 896)
@@ -209,21 +210,21 @@ def tile_picked_shuffle_mlp_none_perm_l_kernel(tc, xT, w1, w2, offs, out):
                 out=w2_first[:, 128 * m : 128 * (m + 1), :].rearrange("p (b i) j -> p b j i", i=4),
                 in_=c0[0][:].rearrange("p j (b i m) -> p m b j i", i=4, m=2)[:, m],
             )
+        quantise_w2h(w2_first, 0, 0)
         gather(0)
         gather(1)
-        quantise_w2h(w2_first, 0, 0)
         quantise_w2h(w2_first, 0, 1)
         turn(0)
         lay("s", 0)
         turn(1)
         lay("s", 1)
-        w2_tile = sb([P, N, J], BF16, "w2_grp", "window")
+        w2_tile = sb([P, N, J], BF16, "w2_grp")
         for m in range(2):
             nc.vector.tensor_copy(
                 out=w2_tile[:, 128 * m : 128 * (m + 1), :].rearrange("p (b i) j -> p b j i", i=4),
                 in_=c1[0][:].rearrange("p j (b i m) -> p m b j i", i=4, m=2)[:, m],
             )
-        hg_cod = sb([P, 2, T], U32, "hg_cod", "c1")
+        hg_cod = sb([P, 2, T], U32, "hg_cod")
         quantise_w2h(w2_tile[:], 1, 0)
         quantise_h(0)
         quantise_w2h(w2_tile[:], 1, 1)

@@ -17,12 +17,14 @@ P = 128
 J = 4
 KP = P * J
 SPLIT = (256, 256)
+CUT = 176
 
 
 def tile_picked_shuffle_mlp_none_perm_l_kernel(tc, xT, w1, w2, offs, out):
     nc = tc.nc
     with ExitStack() as ctx:
         keep = ctx.enter_context(tc.tile_pool(name="keep", bufs=1))
+        placed = ctx.enter_context(tc.tile_pool(name="placed", bufs=1))
         psum = ctx.enter_context(tc.psum_pool(name="psum", bufs=1))
 
         def sb(shape, dtype, name, tag=None):
@@ -48,15 +50,20 @@ def tile_picked_shuffle_mlp_none_perm_l_kernel(tc, xT, w1, w2, offs, out):
 
         offsets = keep.tile([P, H // 16], U16, name="offsets")
         x_raw = sb([P, 2, J, T], F32, "x_raw")
-        a0 = load(w1, "a0", 0, 0, 4, 0, 1024)
-        load_x()
+        lo1 = load(w1, "a", 0, 0, 2, 0, 1024)
+        hi1 = load(w1, "a", 0, 2, 4, 0, 1024, lo1[0])
         lo2 = load(w1, "b", 1, 0, 2, 0, 1024)
+        load_x()
         load(w1, "b", 1, 2, 4, 0, 512, lo2[0])
         load(w1, "b", 1, 2, 4, 512, 768, lo2[0])
         load(w1, "b", 1, 2, 4, 768, 1024, lo2[0])
         c0 = load(w2, "c0", 0, 0, 4, 0, N)
         nc.sync.dma_start(offsets[:], offs)
-        c1 = load(w2, "c1", 1, 0, 4, 0, N)
+        w2_rows = w2[KP:, :].rearrange("(p j) c -> p j c", j=J)
+        c1a = sb([P, J, CUT], F32, "c1a")
+        nc.sync.dma_start(out=c1a[:], in_=w2_rows[:, :, :CUT])
+        c1b = placed.tile([P, J, N - CUT], F32, name="c1b", offset=0, align_bytes=256)
+        nc.sync.dma_start(out=c1b[:], in_=w2_rows[:, :, CUT:])
         hi2 = (lo2[0], 2, 4, 0)
         all4 = (lo2[0], 0, 4, 0)
 
@@ -68,7 +75,7 @@ def tile_picked_shuffle_mlp_none_perm_l_kernel(tc, xT, w1, w2, offs, out):
         x_cod = sb([P, 2, T], U32, "x_cod")
         x_scl = sb([P, 2, T], U8, "x_scl")
 
-        h16 = sb([P, H], BF16, "h16")
+        h16 = sb([P, H], BF16, "h16", "window")
         width = {0: 256, 256: 256, 512: 128, 640: 128, 768: 128, 896: 128}
         banks = {}
         for b in sorted(width):
@@ -143,7 +150,7 @@ def tile_picked_shuffle_mlp_none_perm_l_kernel(tc, xT, w1, w2, offs, out):
             picked[q] = g
 
         turned = {}
-        hg_grp = {}
+        hg_grp = [placed.tile([P, T * J], BF16, name="hg_grp_%d" % q, offset=1024 * q, align_bytes=256) for q in range(2)]
         hg_scl = {}
 
         def turn(q):
@@ -153,25 +160,26 @@ def tile_picked_shuffle_mlp_none_perm_l_kernel(tc, xT, w1, w2, offs, out):
                 nc.tensor.transpose(turned[q][:, u, :], words[:, u : 256 : 2], ident[:])
 
         def lay(engine, q):
-            hg_grp[q] = sb([P, T * J], BF16, "hg_grp_%d" % q)
             copy(engine, hg_grp[q][:].bitcast(F32).rearrange("p (t u) -> p t u", u=2), turned[q][:].rearrange("p u t -> p t u"))
 
         def quantise_h(q):
             hg_scl[q] = sb([P, T], U8, "hg_scl_%d" % q)
             nc.vector.quantize_mx(out=hg_cod[:, q, :].bitcast(FP8X4), scales=hg_scl[q][:], in_=hg_grp[q][:])
 
-        interleave("s", grps[0], a0, 320, 512)
-        interleave("v", grps[0], a0, 0, 320)
-        interleave("s", grps[0], a0, 832, 1024)
-        interleave("v", grps[0], a0, 512, 832)
-        interleave_x("s", 0)
-        interleave_x("v", 1)
+        interleave("s", grps[0], lo1, 672, 1024)
+        interleave("v", grps[0], lo1, 0, 672)
+        interleave("s", grps[0], hi1, 288, 512)
+        interleave("v", grps[0], hi1, 0, 288)
+        interleave("s", grps[0], hi1, 784, 1024)
+        interleave("v", grps[0], hi1, 512, 784)
         quantise(0, 0, 512)
-        quantise_x(1)
         quantise(0, 512, 1024)
-        interleave("s", grps[1], lo2, 128, 496)
-        interleave("v", grps[1], lo2, 496, 1024)
+        interleave("s", grps[1], lo2, 128, 464)
+        interleave("v", grps[1], lo2, 464, 1024)
+        interleave_x("v", 0)
+        interleave_x("s", 1)
         quantise_x(0)
+        quantise_x(1)
         multiply(0, 0)
         multiply(0, 256)
         multiply(0, 512)
@@ -214,16 +222,15 @@ def tile_picked_shuffle_mlp_none_perm_l_kernel(tc, xT, w1, w2, offs, out):
         gather(0)
         gather(1)
         quantise_w2h(w2_first, 0, 1)
+        w2_tile = sb([P, N, J], BF16, "w2_grp")
+        dealt = w2_tile[:].rearrange("p (m b i) j -> p m b j i", m=2, i=4)
+        nc.scalar.copy(out=dealt[:, :, CUT // 8 :], in_=c1b[:].rearrange("p j (b i m) -> p m b j i", i=4, m=2))
         turn(0)
         lay("s", 0)
         turn(1)
         lay("s", 1)
-        w2_tile = sb([P, N, J], BF16, "w2_grp")
         for m in range(2):
-            nc.vector.tensor_copy(
-                out=w2_tile[:, 128 * m : 128 * (m + 1), :].rearrange("p (b i) j -> p b j i", i=4),
-                in_=c1[0][:].rearrange("p j (b i m) -> p m b j i", i=4, m=2)[:, m],
-            )
+            nc.vector.tensor_copy(out=dealt[:, m, : CUT // 8], in_=c1a[:].rearrange("p j (b i m) -> p m b j i", i=4, m=2)[:, m])
         hg_cod = sb([P, 2, T], U32, "hg_cod")
         quantise_w2h(w2_tile[:], 1, 0)
         quantise_h(0)

@@ -1,6 +1,7 @@
+from contextlib import ExitStack
+
 import concourse.mybir as mybir
 from concourse.masks import make_identity
-from contextlib import ExitStack
 
 K, T, H, N = 1024, 128, 1024, 256
 FLOPS = 2 * K * H * T + 2 * H * N * T
@@ -16,8 +17,6 @@ COPY = mybir.ActivationFunctionType.Copy
 P = 128
 J = 4
 KP = P * J
-SPLIT = (256, 256)
-CUT = 176
 
 
 def tile_picked_shuffle_mlp_none_perm_l_kernel(tc, xT, w1, w2, offs, out):
@@ -39,33 +38,35 @@ def tile_picked_shuffle_mlp_none_perm_l_kernel(tc, xT, w1, w2, offs, out):
             else:
                 nc.scalar.copy(out=dst, in_=src)
 
-        def load(w, name, q, j0, j1, c0, c1, into=None):
-            raw = into if into is not None else sb([P, J, w.shape[1]], F32, name)
-            src = w[q * KP : (q + 1) * KP, :].rearrange("(p j) c -> p j c", j=J)
-            nc.sync.dma_start(out=raw[:, j0:j1, c0:c1], in_=src[:, j0:j1, c0:c1])
-            return (raw, j0, j1, c0)
-
-        def load_x():
-            nc.sync.dma_start(out=x_raw[:].rearrange("p q j t -> p q (j t)"), in_=xT.rearrange("(q p j) t -> p q (j t)", q=2, j=J))
+        def rows_of(w, q):
+            return w[q * KP : (q + 1) * KP, :].rearrange("(p j) c -> p j c", j=J)
 
         offsets = keep.tile([P, H // 16], U16, name="offsets")
         x_raw = sb([P, 2, J, T], F32, "x_raw")
-        lo1 = load(w1, "a", 0, 0, 2, 0, 1024)
-        hi1 = load(w1, "a", 0, 2, 4, 0, 1024, lo1[0])
-        lo2 = load(w1, "b", 1, 0, 2, 0, 1024)
-        load_x()
-        load(w1, "b", 1, 2, 4, 0, 512, lo2[0])
-        load(w1, "b", 1, 2, 4, 512, 768, lo2[0])
-        load(w1, "b", 1, 2, 4, 768, 1024, lo2[0])
-        c0 = load(w2, "c0", 0, 0, 4, 0, N)
+        raw = {}
+
+        def load_w1(q, lo, hi):
+            raw[q, lo] = sb([P, J, hi - lo], F32, "w1_raw_%d_%d" % (q, lo))
+            nc.sync.dma_start(out=raw[q, lo][:], in_=rows_of(w1, q)[:, :, lo:hi])
+
+        w2_raw = {}
+
+        def load_w2(q, m, tile):
+            w2_raw[q, m] = tile
+            nc.sync.dma_start(out=tile[:], in_=rows_of(w2, q)[:, :, 128 * m : 128 * (m + 1)])
+
+        load_w1(0, 0, 512)
+        load_w1(0, 512, 1024)
+        nc.sync.dma_start(out=x_raw[:].rearrange("p q j t -> p q (j t)"), in_=xT.rearrange("(q p j) t -> p q (j t)", q=2, j=J))
+        load_w1(1, 0, 512)
+        load_w1(1, 512, 768)
+        load_w1(1, 768, 896)
+        load_w1(1, 896, 1024)
+        load_w2(0, 0, sb([P, J, 128], F32, "w2_raw_0_0"))
+        load_w2(0, 1, sb([P, J, 128], F32, "w2_raw_0_1"))
         nc.sync.dma_start(offsets[:], offs)
-        w2_rows = w2[KP:, :].rearrange("(p j) c -> p j c", j=J)
-        c1a = sb([P, J, CUT], F32, "c1a")
-        nc.sync.dma_start(out=c1a[:], in_=w2_rows[:, :, :CUT])
-        c1b = placed.tile([P, J, N - CUT], F32, name="c1b", offset=0, align_bytes=256)
-        nc.sync.dma_start(out=c1b[:], in_=w2_rows[:, :, CUT:])
-        hi2 = (lo2[0], 2, 4, 0)
-        all4 = (lo2[0], 0, 4, 0)
+        load_w2(1, 1, placed.tile([P, J, 128], F32, name="w2_raw_1_1", offset=0, align_bytes=256))
+        load_w2(1, 0, sb([P, J, 128], F32, "w2_raw_1_0"))
 
         ident = sb([P, P], F32, "ident")
         make_identity(nc, ident[:])
@@ -74,28 +75,19 @@ def tile_picked_shuffle_mlp_none_perm_l_kernel(tc, xT, w1, w2, offs, out):
         x_grp = sb([P, 2 * T, J], BF16, "x_grp")[:]
         x_cod = sb([P, 2, T], U32, "x_cod")
         x_scl = sb([P, 2, T], U8, "x_scl")
+        h16 = sb([P, H], BF16, "window", "w1_raw_1_768")
+        width = {0: 256, 256: 256, 512: 256, 768: 128, 896: 128}
+        banks = {b: ps([P, width[b]], "h_%d" % b, "bank_%d" % b) for b in sorted(width)}
 
-        h16 = sb([P, H], BF16, "h16", "window")
-        width = {0: 256, 256: 256, 512: 128, 640: 128, 768: 128, 896: 128}
-        banks = {}
-        for b in sorted(width):
-            banks[b] = ps([P, width[b]], "h_%d" % b, "bank_%d" % b)
+        def weave(engine, dst, src):
+            copy(engine, dst.rearrange("p (b i) j -> p b j i", i=4), src.rearrange("p j (b i) -> p b j i", i=4))
 
-        def interleave(engine, grp, piece, lo, hi):
-            raw, j0, j1, c0 = piece
-            dst = grp[:, lo:hi, j0:j1]
-            src = raw[:, j0:j1, lo:hi]
-            if j1 - j0 == J:
-                dst = dst.rearrange("p (b i) j -> p b j i", i=4)
-                src = src.rearrange("p j (b i) -> p b j i", i=4)
-            else:
-                src = src.rearrange("p j c -> p c j")
-            copy(engine, dst, src)
+        def interleave(engine, q, piece, lo, hi):
+            weave(engine, grps[q][:, lo:hi, :], raw[q, piece][:, :, lo - piece : hi - piece])
 
         def interleave_x(engine, q):
             dst = x_grp[:, q * T : (q + 1) * T, :].rearrange("p (b i) j -> p b j i", i=4)
-            src = x_raw[:, q].rearrange("p j (b i) -> p b j i", i=4)
-            copy(engine, dst, src)
+            copy(engine, dst, x_raw[:, q].rearrange("p j (b i) -> p b j i", i=4))
 
         def quantise_x(q):
             nc.vector.quantize_mx(
@@ -107,12 +99,11 @@ def tile_picked_shuffle_mlp_none_perm_l_kernel(tc, xT, w1, w2, offs, out):
         made = {}
 
         def quantise(q, lo, hi):
-            n = hi - lo
-            cod = sb([P, n], U32, "w1_cod_%d_%d" % (q, lo))
-            scl = sb([P, n], U8, "w1_scl_%d_%d" % (q, lo))
+            cod = sb([P, hi - lo], U32, "w1_cod_%d_%d" % (q, lo))
+            scl = sb([P, hi - lo], U8, "w1_scl_%d_%d" % (q, lo))
             nc.vector.quantize_mx(out=cod[:].bitcast(FP8X4), scales=scl[:], in_=grps[q][:, lo:hi].rearrange("p c j -> p (c j)"))
-            for c in sorted(width):
-                if lo <= c and c < hi:
+            for c in width:
+                if lo <= c < hi:
                     made[q, c] = (cod, scl, c - lo)
 
         def multiply(q, c):
@@ -133,25 +124,26 @@ def tile_picked_shuffle_mlp_none_perm_l_kernel(tc, xT, w1, w2, offs, out):
         w2_cod = {}
         w2_scl = {}
 
-        def quantise_w2h(grp, q, m):
-            if m == 0:
-                w2_cod[q] = sb([P, N], U32, "w2_cod_%d" % q)
-                w2_scl[q] = sb([P, N], U8, "w2_scl_%d" % q)
-            cols = slice(128 * m, 128 * (m + 1))
-            nc.vector.quantize_mx(out=w2_cod[q][:, cols].bitcast(FP8X4), scales=w2_scl[q][:, cols], in_=grp[:, cols, :].rearrange("p c j -> p (c j)"))
+        w2_grp = {(q, m): sb([P, 128, J], BF16, "w2_grp_%d_%d" % (q, m)) for q in range(2) for m in range(2)}
 
-        picked = {}
+        def interleave_w2(engine, q, m):
+            weave(engine, w2_grp[q, m][:], w2_raw[q, m][:])
+
+        def quantise_w2(q, m, tag=None):
+            w2_cod[q, m] = sb([P, 128], U32, "w2_cod_%d_%d" % (q, m), tag)
+            w2_scl[q, m] = sb([P, 128], U8, "w2_scl_%d_%d" % (q, m))
+            nc.vector.quantize_mx(out=w2_cod[q, m][:].bitcast(FP8X4), scales=w2_scl[q, m][:], in_=w2_grp[q, m][:].rearrange("p c j -> p (c j)"))
+
+        picked = [sb([P, KP], BF16, "picked_%d" % q) for q in range(2)]
 
         def gather(q):
-            g = sb([P, KP], BF16, "picked_%d" % q)
-            s = SPLIT[q]
-            nc.vector.tensor_copy(out=g[:, 0:s], in_=h16[:].indirect(offsets[:, 32 * q : 32 * q + s // 16]))
-            nc.scalar.activation(out=g[:, s:KP], in_=h16[:].indirect(offsets[:, 32 * q + s // 16 : 32 * q + 32]), func=COPY)
-            picked[q] = g
+            nc.vector.tensor_copy(out=picked[q][:, :256], in_=h16[:].indirect(offsets[:, 32 * q : 32 * q + 16]))
+            nc.scalar.activation(out=picked[q][:, 256:], in_=h16[:].indirect(offsets[:, 32 * q + 16 : 32 * q + 32]), func=COPY)
 
         turned = {}
         hg_grp = [placed.tile([P, T * J], BF16, name="hg_grp_%d" % q, offset=1024 * q, align_bytes=256) for q in range(2)]
-        hg_scl = {}
+        hg_cod = sb([P, 2, T], U32, "hg_cod")
+        hg_scl = [sb([P, T], U8, "hg_scl_%d" % q) for q in range(2)]
 
         def turn(q):
             turned[q] = ps([P, 2, T], "turned_%d" % q, "turned_%d" % q)
@@ -159,82 +151,60 @@ def tile_picked_shuffle_mlp_none_perm_l_kernel(tc, xT, w1, w2, offs, out):
             for u in range(2):
                 nc.tensor.transpose(turned[q][:, u, :], words[:, u : 256 : 2], ident[:])
 
-        def lay(engine, q):
-            copy(engine, hg_grp[q][:].bitcast(F32).rearrange("p (t u) -> p t u", u=2), turned[q][:].rearrange("p u t -> p t u"))
+        def lay(q):
+            nc.scalar.copy(out=hg_grp[q][:].bitcast(F32).rearrange("p (t u) -> p t u", u=2), in_=turned[q][:].rearrange("p u t -> p t u"))
 
         def quantise_h(q):
-            hg_scl[q] = sb([P, T], U8, "hg_scl_%d" % q)
             nc.vector.quantize_mx(out=hg_cod[:, q, :].bitcast(FP8X4), scales=hg_scl[q][:], in_=hg_grp[q][:])
 
-        interleave("s", grps[0], lo1, 672, 1024)
-        interleave("v", grps[0], lo1, 0, 672)
-        interleave("s", grps[0], hi1, 288, 512)
-        interleave("v", grps[0], hi1, 0, 288)
-        interleave("s", grps[0], hi1, 784, 1024)
-        interleave("v", grps[0], hi1, 512, 784)
-        quantise(0, 0, 512)
-        quantise(0, 512, 1024)
-        interleave("s", grps[1], lo2, 128, 464)
-        interleave("v", grps[1], lo2, 464, 1024)
+        for piece in (0, 512):
+            interleave("s", 0, piece, piece + 288, piece + 512)
+            interleave("v", 0, piece, piece, piece + 288)
+            quantise(0, piece, piece + 256)
+            quantise(0, piece + 256, piece + 512)
         interleave_x("v", 0)
         interleave_x("s", 1)
         quantise_x(0)
         quantise_x(1)
-        multiply(0, 0)
-        multiply(0, 256)
-        multiply(0, 512)
-        multiply(0, 640)
-        multiply(0, 768)
-        multiply(0, 896)
-        interleave("s", grps[1], hi2, 304, 512)
-        interleave("v", grps[1], all4, 0, 128)
-        interleave("v", grps[1], hi2, 128, 256)
-        interleave("v", grps[1], hi2, 256, 304)
-        interleave("s", grps[1], hi2, 560, 768)
-        interleave("v", grps[1], hi2, 512, 560)
+        for c in sorted(width):
+            multiply(0, c)
+        interleave("s", 1, 0, 256, 512)
+        interleave("v", 1, 0, 0, 256)
         quantise(1, 0, 256)
         multiply(1, 0)
+        interleave("s", 1, 512, 512, 640)
+        interleave("v", 1, 512, 640, 768)
         quantise(1, 256, 512)
         multiply(1, 256)
-        interleave("s", grps[1], hi2, 896, 1024)
-        interleave("v", grps[1], hi2, 768, 896)
-        quantise(1, 512, 640)
+        interleave("s", 1, 768, 768, 864)
+        interleave("v", 1, 768, 864, 896)
+        quantise(1, 512, 768)
         multiply(1, 512)
-        quantise(1, 640, 768)
-        multiply(1, 640)
+        interleave("v", 1, 896, 896, 1024)
         quantise(1, 768, 896)
         multiply(1, 768)
         quantise(1, 896, 1024)
         multiply(1, 896)
         window("s", 0)
+        window("s", 512)
         window("s", 256)
-        window("v", 512)
-        window("s", 640)
         window("s", 768)
         window("s", 896)
-        w2_first = grps[1][:, H - N :, :]
-        for m in range(2):
-            nc.vector.tensor_copy(
-                out=w2_first[:, 128 * m : 128 * (m + 1), :].rearrange("p (b i) j -> p b j i", i=4),
-                in_=c0[0][:].rearrange("p j (b i m) -> p m b j i", i=4, m=2)[:, m],
-            )
-        quantise_w2h(w2_first, 0, 0)
+        interleave_w2("v", 0, 0)
+        quantise_w2(0, 0)
+        interleave_w2("v", 0, 1)
         gather(0)
         gather(1)
-        quantise_w2h(w2_first, 0, 1)
-        w2_tile = sb([P, N, J], BF16, "w2_grp")
-        dealt = w2_tile[:].rearrange("p (m b i) j -> p m b j i", m=2, i=4)
-        nc.scalar.copy(out=dealt[:, :, CUT // 8 :], in_=c1b[:].rearrange("p j (b i m) -> p m b j i", i=4, m=2))
+        quantise_w2(0, 1, "w1_raw_1_768")
+        interleave_w2("s", 1, 1)
         turn(0)
-        lay("s", 0)
+        lay(0)
         turn(1)
-        lay("s", 1)
-        for m in range(2):
-            nc.vector.tensor_copy(out=dealt[:, m, : CUT // 8], in_=c1a[:].rearrange("p j (b i m) -> p m b j i", i=4, m=2)[:, m])
-        hg_cod = sb([P, 2, T], U32, "hg_cod")
-        quantise_w2h(w2_tile[:], 1, 0)
+        lay(1)
+        interleave_w2("v", 1, 0)
+        quantise_w2(1, 1)
+        quantise_w2(1, 0)
         quantise_h(0)
-        quantise_w2h(w2_tile[:], 1, 1)
         quantise_h(1)
 
         accs = [ps([P, T], "acc_%d" % m, "bank_%d" % (256 * m)) for m in range(2)]
@@ -242,8 +212,8 @@ def tile_picked_shuffle_mlp_none_perm_l_kernel(tc, xT, w1, w2, offs, out):
             for m in range(2):
                 nc.tensor.matmul_mx(
                     out=accs[m][:],
-                    lhsT=w2_cod[q][:, 128 * m : 128 * (m + 1)].bitcast(FP8X4),
-                    lhsT_scale=w2_scl[q][:, 128 * m : 128 * (m + 1)],
+                    lhsT=w2_cod[q, m][:].bitcast(FP8X4),
+                    lhsT_scale=w2_scl[q, m][:],
                     rhs=hg_cod[:, q, :].bitcast(FP8X4),
                     rhs_scale=hg_scl[q][:],
                     start=(q == 0),
@@ -252,4 +222,4 @@ def tile_picked_shuffle_mlp_none_perm_l_kernel(tc, xT, w1, w2, offs, out):
         res = sb([P, 2, T], F32, "res")
         nc.vector.tensor_copy(out=res[:, 0, :], in_=accs[0][:])
         nc.scalar.copy(out=res[:, 1, :], in_=accs[1][:])
-        nc.sync.dma_start(out=out.rearrange("(p m) t -> p (m t)", m=2), in_=res[:].rearrange("p m t -> p (m t)"))
+        nc.sync.dma_start(out=out.rearrange("(m p) t -> p m t", m=2), in_=res[:])

@@ -55,8 +55,9 @@ def tile_picked_shuffle_mlp_none_perm_l_kernel(tc, xT, w1, w2, offs, out):
             w2_raw[q, m] = tile
             nc.sync.dma_start(out=tile[:], in_=rows_of(w2, q)[:, :, 128 * m : 128 * (m + 1)])
 
-        load_w1(0, 0, 512)
-        load_w1(0, 512, 1024)
+        raw[0, 0] = sb([P, J, H], F32, "w1_raw_0")
+        for j in (0, 2):
+            nc.sync.dma_start(out=raw[0, 0][:, j : j + 2], in_=rows_of(w1, 0)[:, j : j + 2])
         nc.sync.dma_start(out=x_raw[:].rearrange("p q j t -> p q (j t)"), in_=xT.rearrange("(q p j) t -> p q (j t)", q=2, j=J))
         load_w1(1, 0, 512)
         load_w1(1, 512, 768)
@@ -157,11 +158,17 @@ def tile_picked_shuffle_mlp_none_perm_l_kernel(tc, xT, w1, w2, offs, out):
         def quantise_h(q):
             nc.vector.quantize_mx(out=hg_cod[:, q, :].bitcast(FP8X4), scales=hg_scl[q][:], in_=hg_grp[q][:])
 
-        for piece in (0, 512):
-            interleave("s", 0, piece, piece + 288, piece + 512)
-            interleave("v", 0, piece, piece, piece + 288)
-            quantise(0, piece, piece + 256)
-            quantise(0, piece + 256, piece + 512)
+        def interleave_pair(engine, j, lo, hi):
+            copy(engine, grps[0][:, lo:hi, j : j + 2], raw[0, 0][:, j : j + 2, lo:hi].rearrange("p j c -> p c j"))
+
+        interleave_pair("s", 0, 672, 1024)
+        interleave_pair("v", 0, 0, 672)
+        interleave_pair("s", 2, 288, 512)
+        interleave_pair("v", 2, 0, 288)
+        interleave_pair("s", 2, 784, 1024)
+        interleave_pair("v", 2, 512, 784)
+        quantise(0, 0, 512)
+        quantise(0, 512, 1024)
         interleave_x("v", 0)
         interleave_x("s", 1)
         quantise_x(0)

@@ -193,8 +193,8 @@ def tile_picked_shuffle_mlp_none_perm_l_kernel(tc, xT, w1, w2, offs, out):
         quantise(1, 896, 1024)
         multiply(1, 896)
         window("s", 0)
-        window("s", 512)
         window("s", 256)
+        window("s", 512)
         window("s", 768)
         window("s", 896)
         interleave_w2("v", 0, 0)
@@ -202,7 +202,6 @@ def tile_picked_shuffle_mlp_none_perm_l_kernel(tc, xT, w1, w2, offs, out):
         interleave_w2("v", 0, 1)
         gather(0)
         gather(1)
-        quantise_w2(0, 1, "w1_raw_1_768")
         interleave_w2("s", 1, 1)
         turn(0)
         lay(0)
@@ -210,6 +209,7 @@ def tile_picked_shuffle_mlp_none_perm_l_kernel(tc, xT, w1, w2, offs, out):
         lay(1)
         interleave_w2("v", 1, 0)
         quantise_w2(1, 1)
+        quantise_w2(0, 1, "w2_raw_1_0")
         quantise_w2(1, 0)
         quantise_h(0)
         quantise_h(1)

@@ -55,10 +55,10 @@ def tile_picked_shuffle_mlp_none_perm_l_kernel(tc, xT, w1, w2, offs, out):
             w2_raw[q, m] = tile
             nc.sync.dma_start(out=tile[:], in_=rows_of(w2, q)[:, :, 128 * m : 128 * (m + 1)])
 
+        nc.scalar.dma_start(out=x_raw[:].rearrange("p q j t -> p q (j t)"), in_=xT.rearrange("(q p j) t -> p q (j t)", q=2, j=J))
         raw[0, 0] = sb([P, J, H], F32, "w1_raw_0")
         for j in (0, 2):
-            nc.sync.dma_start(out=raw[0, 0][:, j : j + 2], in_=rows_of(w1, 0)[:, j : j + 2])
-        nc.sync.dma_start(out=x_raw[:].rearrange("p q j t -> p q (j t)"), in_=xT.rearrange("(q p j) t -> p q (j t)", q=2, j=J))
+            nc.sync.dma_start(out=raw[0, 0][:, j : j + 2], in_=rows_of(w1, 0)[:, j : j + 2], max_dma_last_dim=2048)
         load_w1(1, 0, 512)
         load_w1(1, 512, 768)
         load_w1(1, 768, 896)
@@ -161,18 +161,17 @@ def tile_picked_shuffle_mlp_none_perm_l_kernel(tc, xT, w1, w2, offs, out):
         def interleave_pair(engine, j, lo, hi):
             copy(engine, grps[0][:, lo:hi, j : j + 2], raw[0, 0][:, j : j + 2, lo:hi].rearrange("p j c -> p c j"))
 
-        interleave_pair("s", 0, 672, 1024)
-        interleave_pair("v", 0, 0, 672)
-        interleave_pair("s", 2, 288, 512)
-        interleave_pair("v", 2, 0, 288)
-        interleave_pair("s", 2, 784, 1024)
-        interleave_pair("v", 2, 512, 784)
-        quantise(0, 0, 512)
-        quantise(0, 512, 1024)
         interleave_x("v", 0)
         interleave_x("s", 1)
         quantise_x(0)
         quantise_x(1)
+        interleave_pair("s", 0, 672, 1024)
+        interleave_pair("v", 0, 0, 672)
+        for c in (0, 512):
+            interleave_pair("s", 2, c + 256, c + 512)
+            interleave_pair("v", 2, c, c + 256)
+        for c in range(0, H, 256):
+            quantise(0, c, c + 256)
         for c in sorted(width):
             multiply(0, c)
         interleave("s", 1, 0, 256, 512)

@@ -66,8 +66,8 @@ def tile_picked_shuffle_mlp_none_perm_l_kernel(tc, xT, w1, w2, offs, out):
         load_w2(0, 0, sb([P, J, 128], F32, "w2_raw_0_0"))
         load_w2(0, 1, sb([P, J, 128], F32, "w2_raw_0_1"))
         nc.sync.dma_start(offsets[:], offs)
-        load_w2(1, 1, placed.tile([P, J, 128], F32, name="w2_raw_1_1", offset=0, align_bytes=256))
         load_w2(1, 0, sb([P, J, 128], F32, "w2_raw_1_0"))
+        load_w2(1, 1, placed.tile([P, J, 128], F32, name="w2_raw_1_1", offset=0, align_bytes=256))
 
         ident = sb([P, P], F32, "ident")
         make_identity(nc, ident[:])
@@ -207,9 +207,9 @@ def tile_picked_shuffle_mlp_none_perm_l_kernel(tc, xT, w1, w2, offs, out):
         turn(1)
         lay(1)
         interleave_w2("v", 1, 0)
-        quantise_w2(1, 1)
         quantise_w2(0, 1, "w2_raw_1_0")
         quantise_w2(1, 0)
+        quantise_w2(1, 1)
         quantise_h(0)
         quantise_h(1)
 

@@ -56,9 +56,8 @@ def tile_picked_shuffle_mlp_none_perm_l_kernel(tc, xT, w1, w2, offs, out):
             nc.sync.dma_start(out=tile[:], in_=rows_of(w2, q)[:, :, 128 * m : 128 * (m + 1)])
 
         nc.scalar.dma_start(out=x_raw[:].rearrange("p q j t -> p q (j t)"), in_=xT.rearrange("(q p j) t -> p q (j t)", q=2, j=J))
-        raw[0, 0] = sb([P, J, H], F32, "w1_raw_0")
-        for j in (0, 2):
-            nc.sync.dma_start(out=raw[0, 0][:, j : j + 2], in_=rows_of(w1, 0)[:, j : j + 2], max_dma_last_dim=2048)
+        load_w1(0, 0, 512)
+        load_w1(0, 512, 1024)
         load_w1(1, 0, 512)
         load_w1(1, 512, 768)
         load_w1(1, 768, 896)
@@ -74,8 +73,8 @@ def tile_picked_shuffle_mlp_none_perm_l_kernel(tc, xT, w1, w2, offs, out):
 
         grps = [sb([P, H, J], BF16, "w1_grp_%d" % q) for q in range(2)]
         x_grp = sb([P, 2 * T, J], BF16, "x_grp")[:]
-        x_cod = sb([P, 2, T], U32, "x_cod")
-        x_scl = sb([P, 2, T], U8, "x_scl")
+        x_cod = {}
+        x_scl = {}
         h16 = sb([P, H], BF16, "window", "w1_raw_1_768")
         width = {0: 256, 256: 256, 512: 256, 768: 128, 896: 128}
         banks = {b: ps([P, width[b]], "h_%d" % b, "bank_%d" % b) for b in sorted(width)}
@@ -90,10 +89,12 @@ def tile_picked_shuffle_mlp_none_perm_l_kernel(tc, xT, w1, w2, offs, out):
             dst = x_grp[:, q * T : (q + 1) * T, :].rearrange("p (b i) j -> p b j i", i=4)
             copy(engine, dst, x_raw[:, q].rearrange("p j (b i) -> p b j i", i=4))
 
-        def quantise_x(q):
+        def quantise_x(q, tag=None):
+            x_cod[q] = sb([P, T], U32, "x_cod_%d" % q, tag)
+            x_scl[q] = sb([P, T], U8, "x_scl_%d" % q)
             nc.vector.quantize_mx(
-                out=x_cod[:, q, :].bitcast(FP8X4),
-                scales=x_scl[:, q, :],
+                out=x_cod[q][:].bitcast(FP8X4),
+                scales=x_scl[q][:],
                 in_=x_grp[:, q * T : (q + 1) * T, :].rearrange("p c j -> p (c j)"),
             )
 
@@ -111,8 +112,8 @@ def tile_picked_shuffle_mlp_none_perm_l_kernel(tc, xT, w1, w2, offs, out):
             cod, scl, a = made[q, c]
             nc.tensor.matmul_mx(
                 out=banks[c][:],
-                lhsT=x_cod[:, q, :].bitcast(FP8X4),
-                lhsT_scale=x_scl[:, q, :],
+                lhsT=x_cod[q][:].bitcast(FP8X4),
+                lhsT_scale=x_scl[q][:],
                 rhs=cod[:, a : a + width[c]].bitcast(FP8X4),
                 rhs_scale=scl[:, a : a + width[c]],
                 start=(q == 0),
@@ -125,15 +126,18 @@ def tile_picked_shuffle_mlp_none_perm_l_kernel(tc, xT, w1, w2, offs, out):
         w2_cod = {}
         w2_scl = {}
 
-        w2_grp = {(q, m): sb([P, 128, J], BF16, "w2_grp_%d_%d" % (q, m)) for q in range(2) for m in range(2)}
+        w2_grp = [sb([P, N, J], BF16, "w2_grp_%d" % q) for q in range(2)]
 
         def interleave_w2(engine, q, m):
-            weave(engine, w2_grp[q, m][:], w2_raw[q, m][:])
+            weave(engine, w2_grp[q][:, 128 * m : 128 * (m + 1)], w2_raw[q, m][:])
 
-        def quantise_w2(q, m, tag=None):
-            w2_cod[q, m] = sb([P, 128], U32, "w2_cod_%d_%d" % (q, m), tag)
-            w2_scl[q, m] = sb([P, 128], U8, "w2_scl_%d_%d" % (q, m))
-            nc.vector.quantize_mx(out=w2_cod[q, m][:].bitcast(FP8X4), scales=w2_scl[q, m][:], in_=w2_grp[q, m][:].rearrange("p c j -> p (c j)"))
+        def quantise_w2(q, lo, hi, tag=None):
+            cod = sb([P, hi - lo], U32, "w2_cod_%d_%d" % (q, lo), tag)
+            scl = sb([P, hi - lo], U8, "w2_scl_%d_%d" % (q, lo))
+            nc.vector.quantize_mx(out=cod[:].bitcast(FP8X4), scales=scl[:], in_=w2_grp[q][:, lo:hi].rearrange("p c j -> p (c j)"))
+            for c in range(lo, hi, 128):
+                w2_cod[q, c // 128] = cod[:, c - lo : c - lo + 128]
+                w2_scl[q, c // 128] = scl[:, c - lo : c - lo + 128]
 
         picked = [sb([P, KP], BF16, "picked_%d" % q) for q in range(2)]
 
@@ -158,20 +162,15 @@ def tile_picked_shuffle_mlp_none_perm_l_kernel(tc, xT, w1, w2, offs, out):
         def quantise_h(q):
             nc.vector.quantize_mx(out=hg_cod[:, q, :].bitcast(FP8X4), scales=hg_scl[q][:], in_=hg_grp[q][:])
 
-        def interleave_pair(engine, j, lo, hi):
-            copy(engine, grps[0][:, lo:hi, j : j + 2], raw[0, 0][:, j : j + 2, lo:hi].rearrange("p j c -> p c j"))
-
         interleave_x("v", 0)
         interleave_x("s", 1)
-        quantise_x(0)
         quantise_x(1)
-        interleave_pair("s", 0, 672, 1024)
-        interleave_pair("v", 0, 0, 672)
-        for c in (0, 512):
-            interleave_pair("s", 2, c + 256, c + 512)
-            interleave_pair("v", 2, c, c + 256)
-        for c in range(0, H, 256):
-            quantise(0, c, c + 256)
+        for piece in (0, 512):
+            interleave("s", 0, piece, piece + 256, piece + 512)
+            interleave("v", 0, piece, piece, piece + 256)
+            quantise(0, piece, piece + 256)
+            quantise(0, piece + 256, piece + 512)
+        quantise_x(0, "w1_grp_0")
         for c in sorted(width):
             multiply(0, c)
         interleave("s", 1, 0, 256, 512)
@@ -197,7 +196,6 @@ def tile_picked_shuffle_mlp_none_perm_l_kernel(tc, xT, w1, w2, offs, out):
         window("s", 768)
         window("s", 896)
         interleave_w2("v", 0, 0)
-        quantise_w2(0, 0)
         interleave_w2("v", 0, 1)
         gather(0)
         gather(1)
@@ -207,9 +205,9 @@ def tile_picked_shuffle_mlp_none_perm_l_kernel(tc, xT, w1, w2, offs, out):
         turn(1)
         lay(1)
         interleave_w2("v", 1, 0)
-        quantise_w2(0, 1, "w2_raw_1_0")
-        quantise_w2(1, 0)
-        quantise_w2(1, 1)
+        quantise_w2(0, 0, 256, "w2_raw_1_0")
+        quantise_w2(1, 0, 128)
+        quantise_w2(1, 128, 256)
         quantise_h(0)
         quantise_h(1)
 
@@ -218,8 +216,8 @@ def tile_picked_shuffle_mlp_none_perm_l_kernel(tc, xT, w1, w2, offs, out):
             for m in range(2):
                 nc.tensor.matmul_mx(
                     out=accs[m][:],
-                    lhsT=w2_cod[q, m][:].bitcast(FP8X4),
-                    lhsT_scale=w2_scl[q, m][:],
+                    lhsT=w2_cod[q, m].bitcast(FP8X4),
+                    lhsT_scale=w2_scl[q, m],
                     rhs=hg_cod[:, q, :].bitcast(FP8X4),
                     rhs_scale=hg_scl[q][:],
                     start=(q == 0),

@@ -17,6 +17,13 @@ COPY = mybir.ActivationFunctionType.Copy
 P = 128
 J = 4
 KP = P * J
+M = 128
+
+FIRST_PASS = (0, 512)
+SECOND_PASS = (0, 512, 768, 896)
+BANKS = {0: 256, 256: 256, 512: 256, 768: 128, 896: 128}
+SCALAR_HEAD = {512: 104, 768: 96}
+CUT = 176
 
 
 def tile_picked_shuffle_mlp_none_perm_l_kernel(tc, xT, w1, w2, offs, out):
@@ -26,204 +33,148 @@ def tile_picked_shuffle_mlp_none_perm_l_kernel(tc, xT, w1, w2, offs, out):
         placed = ctx.enter_context(tc.tile_pool(name="placed", bufs=1))
         psum = ctx.enter_context(tc.psum_pool(name="psum", bufs=1))
 
-        def sb(shape, dtype, name, tag=None):
-            return keep.tile(shape, dtype, name=name, tag=tag or name, align_bytes=256)
+        def sbuf(shape, dtype, name, on=None):
+            return keep.tile(shape, dtype, name=name, tag=on or name, align_bytes=256)
 
-        def ps(shape, name, tag):
-            return psum.tile(shape, F32, name=name, tag=tag)
+        def on_vector(dst, src):
+            nc.vector.tensor_copy(out=dst, in_=src)
 
-        def copy(engine, dst, src):
-            if engine == "v":
-                nc.vector.tensor_copy(out=dst, in_=src)
-            else:
-                nc.scalar.copy(out=dst, in_=src)
+        def on_scalar(dst, src):
+            nc.scalar.copy(out=dst, in_=src)
 
         def rows_of(w, q):
             return w[q * KP : (q + 1) * KP, :].rearrange("(p j) c -> p j c", j=J)
 
-        offsets = keep.tile([P, H // 16], U16, name="offsets")
-        x_raw = sb([P, 2, J, T], F32, "x_raw")
-        raw = {}
+        def interleave(copy, dst, src):
+            copy(dst.rearrange("p (b i) j -> p b j i", i=4), src.rearrange("p j (b i) -> p b j i", i=4))
 
-        def load_w1(q, lo, hi):
-            raw[q, lo] = sb([P, J, hi - lo], F32, "w1_raw_%d_%d" % (q, lo))
-            nc.sync.dma_start(out=raw[q, lo][:], in_=rows_of(w1, q)[:, :, lo:hi])
+        def quantise(name, grouped, on=None):
+            columns = grouped.shape[1]
+            codes = sbuf([P, columns], U32, name + "_codes", on)
+            scales = sbuf([P, columns], U8, name + "_scales")
+            nc.vector.quantize_mx(out=codes[:].bitcast(FP8X4), scales=scales[:], in_=grouped.rearrange("p c j -> p (c j)"))
+            return codes, scales
 
-        w2_raw = {}
-
-        def load_w2(q, m, tile):
-            w2_raw[q, m] = tile
-            nc.sync.dma_start(out=tile[:], in_=rows_of(w2, q)[:, :, 128 * m : 128 * (m + 1)])
-
-        nc.scalar.dma_start(out=x_raw[:].rearrange("p q j t -> p q (j t)"), in_=xT.rearrange("(q p j) t -> p q (j t)", q=2, j=J))
-        load_w1(0, 0, 512)
-        load_w1(0, 512, 1024)
-        load_w1(1, 0, 512)
-        load_w1(1, 512, 768)
-        load_w1(1, 768, 896)
-        load_w1(1, 896, 1024)
-        load_w2(0, 0, sb([P, J, 128], F32, "w2_raw_0_0"))
-        load_w2(0, 1, sb([P, J, 128], F32, "w2_raw_0_1"))
-        nc.sync.dma_start(offsets[:], offs)
-        load_w2(1, 0, sb([P, J, 128], F32, "w2_raw_1_0"))
-        load_w2(1, 1, placed.tile([P, J, 128], F32, name="w2_raw_1_1", offset=0, align_bytes=256))
-
-        ident = sb([P, P], F32, "ident")
-        make_identity(nc, ident[:])
-
-        grps = [sb([P, H, J], BF16, "w1_grp_%d" % q) for q in range(2)]
-        x_grp = sb([P, 2 * T, J], BF16, "x_grp")[:]
-        x_cod = {}
-        x_scl = {}
-        h16 = sb([P, H], BF16, "window", "w1_raw_1_768")
-        width = {0: 256, 256: 256, 512: 256, 768: 128, 896: 128}
-        banks = {b: ps([P, width[b]], "h_%d" % b, "bank_%d" % b) for b in sorted(width)}
-
-        def weave(engine, dst, src):
-            copy(engine, dst.rearrange("p (b i) j -> p b j i", i=4), src.rearrange("p j (b i) -> p b j i", i=4))
-
-        def interleave(engine, q, piece, lo, hi):
-            weave(engine, grps[q][:, lo:hi, :], raw[q, piece][:, :, lo - piece : hi - piece])
-
-        def interleave_x(engine, q):
-            dst = x_grp[:, q * T : (q + 1) * T, :].rearrange("p (b i) j -> p b j i", i=4)
-            copy(engine, dst, x_raw[:, q].rearrange("p j (b i) -> p b j i", i=4))
-
-        def quantise_x(q, tag=None):
-            x_cod[q] = sb([P, T], U32, "x_cod_%d" % q, tag)
-            x_scl[q] = sb([P, T], U8, "x_scl_%d" % q)
-            nc.vector.quantize_mx(
-                out=x_cod[q][:].bitcast(FP8X4),
-                scales=x_scl[q][:],
-                in_=x_grp[:, q * T : (q + 1) * T, :].rearrange("p c j -> p (c j)"),
-            )
-
-        made = {}
-
-        def quantise(q, lo, hi):
-            cod = sb([P, hi - lo], U32, "w1_cod_%d_%d" % (q, lo))
-            scl = sb([P, hi - lo], U8, "w1_scl_%d_%d" % (q, lo))
-            nc.vector.quantize_mx(out=cod[:].bitcast(FP8X4), scales=scl[:], in_=grps[q][:, lo:hi].rearrange("p c j -> p (c j)"))
-            for c in width:
-                if lo <= c < hi:
-                    made[q, c] = (cod, scl, c - lo)
-
-        def multiply(q, c):
-            cod, scl, a = made[q, c]
+        def multiply(acc, stationary, moving, q):
             nc.tensor.matmul_mx(
-                out=banks[c][:],
-                lhsT=x_cod[q][:].bitcast(FP8X4),
-                lhsT_scale=x_scl[q][:],
-                rhs=cod[:, a : a + width[c]].bitcast(FP8X4),
-                rhs_scale=scl[:, a : a + width[c]],
+                out=acc,
+                lhsT=stationary[0].bitcast(FP8X4),
+                lhsT_scale=stationary[1],
+                rhs=moving[0].bitcast(FP8X4),
+                rhs_scale=moving[1],
                 start=(q == 0),
                 stop=(q == 1),
             )
 
-        def window(engine, b):
-            copy(engine, h16[:, b : b + width[b]], banks[b][:])
+        offsets = keep.tile([P, H // 16], U16, name="offsets")
+        x_raw = sbuf([P, 2, J, T], F32, "x_raw")
+        nc.scalar.dma_start(
+            out=x_raw[:].rearrange("p q j t -> p q (j t)"),
+            in_=xT.rearrange("(q p j) t -> p q (j t)", q=2, j=J),
+        )
+        w1_raw = {}
+        for q, starts in enumerate((FIRST_PASS, SECOND_PASS)):
+            for lo, hi in zip(starts, starts[1:] + (H,)):
+                w1_raw[q, lo] = sbuf([P, J, hi - lo], F32, "w1_raw_%d_%d" % (q, lo))
+                nc.sync.dma_start(out=w1_raw[q, lo][:], in_=rows_of(w1, q)[:, :, lo:hi])
+        w2_first = []
+        for m in range(2):
+            w2_first.append(sbuf([P, J, M], F32, "w2_first_%d" % m))
+            nc.sync.dma_start(out=w2_first[m][:], in_=rows_of(w2, 0)[:, :, M * m : M * (m + 1)])
+        nc.sync.dma_start(offsets[:], offs)
+        w2_left = sbuf([P, J, CUT], F32, "w2_left")
+        nc.sync.dma_start(out=w2_left[:], in_=rows_of(w2, 1)[:, :, :CUT])
+        w2_right = placed.tile([P, J, N - CUT], F32, name="w2_right", offset=0, align_bytes=256)
+        nc.sync.dma_start(out=w2_right[:], in_=rows_of(w2, 1)[:, :, CUT:])
 
-        w2_cod = {}
-        w2_scl = {}
+        identity = sbuf([P, P], F32, "identity")
+        make_identity(nc, identity[:])
 
-        w2_grp = [sb([P, N, J], BF16, "w2_grp_%d" % q) for q in range(2)]
+        w1_grouped = [sbuf([P, H, J], BF16, "w1_grouped_%d" % q) for q in range(2)]
+        x_grouped = sbuf([P, 2 * T, J], BF16, "x_grouped")
+        window = sbuf([P, H], BF16, "window", on="w1_raw_1_%d" % SECOND_PASS[-2])
+        h_banks = {c: psum.tile([P, n], F32, name="h_%d" % c, tag="bank_%d" % c) for c, n in BANKS.items()}
+        w2_grouped = [sbuf([P, N, J], BF16, "w2_grouped_%d" % q) for q in range(2)]
+        picked = [sbuf([P, KP], BF16, "picked_%d" % q) for q in range(2)]
+        h_grouped = [placed.tile([P, T * J], BF16, name="h_grouped_%d" % q, offset=2 * T * J * q, align_bytes=256) for q in range(2)]
+        h_codes = sbuf([P, 2, T], U32, "h_codes")
+        h_scales = [sbuf([P, T], U8, "h_scales_%d" % q) for q in range(2)]
 
-        def interleave_w2(engine, q, m):
-            weave(engine, w2_grp[q][:, 128 * m : 128 * (m + 1)], w2_raw[q, m][:])
+        x_mx = {}
+        w1_mx = {}
 
-        def quantise_w2(q, lo, hi, tag=None):
-            cod = sb([P, hi - lo], U32, "w2_cod_%d_%d" % (q, lo), tag)
-            scl = sb([P, hi - lo], U8, "w2_scl_%d_%d" % (q, lo))
-            nc.vector.quantize_mx(out=cod[:].bitcast(FP8X4), scales=scl[:], in_=w2_grp[q][:, lo:hi].rearrange("p c j -> p (c j)"))
-            for c in range(lo, hi, 128):
-                w2_cod[q, c // 128] = cod[:, c - lo : c - lo + 128]
-                w2_scl[q, c // 128] = scl[:, c - lo : c - lo + 128]
+        def interleave_w1(copy, q, piece, lo, hi):
+            interleave(copy, w1_grouped[q][:, lo:hi, :], w1_raw[q, piece][:, :, lo - piece : hi - piece])
 
-        picked = [sb([P, KP], BF16, "picked_%d" % q) for q in range(2)]
+        def quantise_x(q, on=None):
+            codes, scales = quantise("x_%d" % q, x_grouped[:, q * T : (q + 1) * T, :], on)
+            x_mx[q] = (codes[:], scales[:])
 
-        def gather(q):
-            nc.vector.tensor_copy(out=picked[q][:, :256], in_=h16[:].indirect(offsets[:, 32 * q : 32 * q + 16]))
-            nc.scalar.activation(out=picked[q][:, 256:], in_=h16[:].indirect(offsets[:, 32 * q + 16 : 32 * q + 32]), func=COPY)
+        def quantise_w1(q, lo, hi):
+            codes, scales = quantise("w1_%d_%d" % (q, lo), w1_grouped[q][:, lo:hi])
+            for c, n in BANKS.items():
+                if lo <= c < hi:
+                    w1_mx[q, c] = (codes[:, c - lo : c - lo + n], scales[:, c - lo : c - lo + n])
 
-        turned = {}
-        hg_grp = [placed.tile([P, T * J], BF16, name="hg_grp_%d" % q, offset=1024 * q, align_bytes=256) for q in range(2)]
-        hg_cod = sb([P, 2, T], U32, "hg_cod")
-        hg_scl = [sb([P, T], U8, "hg_scl_%d" % q) for q in range(2)]
+        def close_bank(c):
+            quantise_w1(1, c, c + BANKS[c])
+            multiply(h_banks[c][:], x_mx[1], w1_mx[1, c], 1)
 
-        def turn(q):
-            turned[q] = ps([P, 2, T], "turned_%d" % q, "turned_%d" % q)
+        for q, copy in enumerate((on_vector, on_scalar)):
+            interleave(copy, x_grouped[:, q * T : (q + 1) * T, :], x_raw[:, q])
+        quantise_x(1)
+        for piece in FIRST_PASS:
+            interleave_w1(on_scalar, 0, piece, piece + 256, piece + 512)
+            interleave_w1(on_vector, 0, piece, piece, piece + 256)
+            quantise_w1(0, piece, piece + 256)
+            quantise_w1(0, piece + 256, piece + 512)
+        quantise_x(0, on="w1_grouped_0")
+        for c in BANKS:
+            multiply(h_banks[c][:], x_mx[0], w1_mx[0, c], 0)
+
+        interleave_w1(on_scalar, 1, 0, 256, 512)
+        interleave_w1(on_vector, 1, 0, 0, 256)
+        close_bank(0)
+        for piece, behind in ((512, 256), (768, 512)):
+            head = piece + SCALAR_HEAD[piece]
+            interleave_w1(on_scalar, 1, piece, piece, head)
+            interleave_w1(on_vector, 1, piece, head, piece + BANKS[piece])
+            close_bank(behind)
+        interleave_w1(on_vector, 1, 896, 896, H)
+        close_bank(768)
+        close_bank(896)
+        for c, n in BANKS.items():
+            on_scalar(window[:, c : c + n], h_banks[c][:])
+
+        for m in range(2):
+            interleave(on_vector, w2_grouped[0][:, M * m : M * (m + 1)], w2_first[m][:])
+        for q in range(2):
+            nc.vector.tensor_copy(out=picked[q][:, :256], in_=window[:].indirect(offsets[:, 32 * q : 32 * q + 16]))
+            nc.scalar.activation(out=picked[q][:, 256:], in_=window[:].indirect(offsets[:, 32 * q + 16 : 32 * q + 32]), func=COPY)
+        interleave(on_scalar, w2_grouped[1][:, CUT:], w2_right[:])
+
+        for q in range(2):
+            turned = psum.tile([P, 2, T], F32, name="turned_%d" % q, tag="turned_%d" % q)
             words = picked[q][:].bitcast(F32)
             for u in range(2):
-                nc.tensor.transpose(turned[q][:, u, :], words[:, u : 256 : 2], ident[:])
+                nc.tensor.transpose(turned[:, u, :], words[:, u : KP // 2 : 2], identity[:])
+            on_scalar(h_grouped[q][:].bitcast(F32).rearrange("p (t u) -> p t u", u=2), turned[:].rearrange("p u t -> p t u"))
 
-        def lay(q):
-            nc.scalar.copy(out=hg_grp[q][:].bitcast(F32).rearrange("p (t u) -> p t u", u=2), in_=turned[q][:].rearrange("p u t -> p t u"))
+        for lo, hi in ((0, M), (M, CUT)):
+            interleave(on_vector, w2_grouped[1][:, lo:hi], w2_left[:, :, lo:hi])
+        w2_mx = {}
+        for q, lo, hi, on in ((1, 0, M, None), (0, 0, N, "w2_left"), (1, M, N, None)):
+            codes, scales = quantise("w2_%d_%d" % (q, lo), w2_grouped[q][:, lo:hi], on)
+            for c in range(lo, hi, M):
+                w2_mx[q, c // M] = (codes[:, c - lo : c - lo + M], scales[:, c - lo : c - lo + M])
+        for q in range(2):
+            nc.vector.quantize_mx(out=h_codes[:, q, :].bitcast(FP8X4), scales=h_scales[q][:], in_=h_grouped[q][:])
 
-        def quantise_h(q):
-            nc.vector.quantize_mx(out=hg_cod[:, q, :].bitcast(FP8X4), scales=hg_scl[q][:], in_=hg_grp[q][:])
-
-        interleave_x("v", 0)
-        interleave_x("s", 1)
-        quantise_x(1)
-        for piece in (0, 512):
-            interleave("s", 0, piece, piece + 256, piece + 512)
-            interleave("v", 0, piece, piece, piece + 256)
-            quantise(0, piece, piece + 256)
-            quantise(0, piece + 256, piece + 512)
-        quantise_x(0, "w1_grp_0")
-        for c in sorted(width):
-            multiply(0, c)
-        interleave("s", 1, 0, 256, 512)
-        interleave("v", 1, 0, 0, 256)
-        quantise(1, 0, 256)
-        multiply(1, 0)
-        interleave("s", 1, 512, 512, 640)
-        interleave("v", 1, 512, 640, 768)
-        quantise(1, 256, 512)
-        multiply(1, 256)
-        interleave("s", 1, 768, 768, 864)
-        interleave("v", 1, 768, 864, 896)
-        quantise(1, 512, 768)
-        multiply(1, 512)
-        interleave("v", 1, 896, 896, 1024)
-        quantise(1, 768, 896)
-        multiply(1, 768)
-        quantise(1, 896, 1024)
-        multiply(1, 896)
-        window("s", 0)
-        window("s", 256)
-        window("s", 512)
-        window("s", 768)
-        window("s", 896)
-        interleave_w2("v", 0, 0)
-        interleave_w2("v", 0, 1)
-        gather(0)
-        gather(1)
-        interleave_w2("s", 1, 1)
-        turn(0)
-        lay(0)
-        turn(1)
-        lay(1)
-        interleave_w2("v", 1, 0)
-        quantise_w2(0, 0, 256, "w2_raw_1_0")
-        quantise_w2(1, 0, 128)
-        quantise_w2(1, 128, 256)
-        quantise_h(0)
-        quantise_h(1)
-
-        accs = [ps([P, T], "acc_%d" % m, "bank_%d" % (256 * m)) for m in range(2)]
+        sums = [psum.tile([P, T], F32, name="sum_%d" % m, tag="bank_%d" % c) for m, c in enumerate((0, 256))]
         for q in range(2):
             for m in range(2):
-                nc.tensor.matmul_mx(
-                    out=accs[m][:],
-                    lhsT=w2_cod[q, m].bitcast(FP8X4),
-                    lhsT_scale=w2_scl[q, m],
-                    rhs=hg_cod[:, q, :].bitcast(FP8X4),
-                    rhs_scale=hg_scl[q][:],
-                    start=(q == 0),
-                    stop=(q == 1),
-                )
-        res = sb([P, 2, T], F32, "res")
-        nc.vector.tensor_copy(out=res[:, 0, :], in_=accs[0][:])
-        nc.scalar.copy(out=res[:, 1, :], in_=accs[1][:])
-        nc.sync.dma_start(out=out.rearrange("(m p) t -> p m t", m=2), in_=res[:])
+                multiply(sums[m][:], w2_mx[q, m], (h_codes[:, q, :], h_scales[q][:]), q)
+        result = sbuf([P, 2, T], F32, "result")
+        on_vector(result[:, 0, :], sums[0][:])
+        on_scalar(result[:, 1, :], sums[1][:])
+        nc.sync.dma_start(out=out.rearrange("(m p) t -> p m t", m=2), in_=result[:])

@@ -140,14 +140,29 @@ def tile_picked_shuffle_mlp_none_perm_l_kernel(tc, xT, w1, w2, offs, out):
             interleave_w1(on_scalar, 1, piece, piece, head)
             interleave_w1(on_vector, 1, piece, head, piece + BANKS[piece])
             close_bank(behind)
-        interleave_w1(on_vector, 1, 896, 896, H)
+        interleave_w1(on_vector, 1, 896, 896, 960)
+        interleave_w1(on_scalar, 1, 896, 960, H)
         close_bank(768)
-        close_bank(896)
+        codes = sbuf([P, 128], U32, "w1_last_codes")
+        scales = sbuf([P, 128], U8, "w1_last_scales")
+        for lo in (0, 64):
+            nc.vector.quantize_mx(out=codes[:, lo : lo + 64].bitcast(FP8X4), scales=scales[:, lo : lo + 64], in_=w1_grouped[1][:, 896 + lo : 960 + lo].rearrange("p c j -> p (c j)"))
+        multiply(h_banks[896][:], x_mx[1], (codes[:], scales[:]), 1)
         for c, n in BANKS.items():
             on_scalar(window[:, c : c + n], h_banks[c][:])
 
-        for m in range(2):
-            interleave(on_vector, w2_grouped[0][:, M * m : M * (m + 1)], w2_first[m][:])
+        w2_mx = {}
+
+        def quantise_w2(q, m, on=None):
+            codes, scales = quantise("w2_%d_%d" % (q, m), w2_grouped[q][:, M * m : M * (m + 1)], on)
+            w2_mx[q, m] = (codes[:], scales[:])
+
+        def quantise_h(q):
+            nc.vector.quantize_mx(out=h_codes[:, q, :].bitcast(FP8X4), scales=h_scales[q][:], in_=h_grouped[q][:])
+
+        interleave(on_vector, w2_grouped[0][:, :M], w2_first[0][:])
+        quantise_w2(0, 0)
+        interleave(on_vector, w2_grouped[0][:, M:], w2_first[1][:])
         for q in range(2):
             nc.vector.tensor_copy(out=picked[q][:, :256], in_=window[:].indirect(offsets[:, 32 * q : 32 * q + 16]))
             nc.scalar.activation(out=picked[q][:, 256:], in_=window[:].indirect(offsets[:, 32 * q + 16 : 32 * q + 32]), func=COPY)
@@ -162,13 +177,11 @@ def tile_picked_shuffle_mlp_none_perm_l_kernel(tc, xT, w1, w2, offs, out):
 
         for lo, hi in ((0, M), (M, CUT)):
             interleave(on_vector, w2_grouped[1][:, lo:hi], w2_left[:, :, lo:hi])
-        w2_mx = {}
-        for q, lo, hi, on in ((1, 0, M, None), (0, 0, N, "w2_left"), (1, M, N, None)):
-            codes, scales = quantise("w2_%d_%d" % (q, lo), w2_grouped[q][:, lo:hi], on)
-            for c in range(lo, hi, M):
-                w2_mx[q, c // M] = (codes[:, c - lo : c - lo + M], scales[:, c - lo : c - lo + M])
-        for q in range(2):
-            nc.vector.quantize_mx(out=h_codes[:, q, :].bitcast(FP8X4), scales=h_scales[q][:], in_=h_grouped[q][:])
+        quantise_w2(1, 0)
+        quantise_w2(0, 1, "w2_left")
+        quantise_h(0)
+        quantise_w2(1, 1, "picked_1")
+        quantise_h(1)
 
         sums = [psum.tile([P, T], F32, name="sum_%d" % m, tag="bank_%d" % c) for m, c in enumerate((0, 256))]
         for q in range(2):

@@ -23,7 +23,7 @@ FIRST_PASS = (0, 512)
 SECOND_PASS = (0, 512, 768, 896)
 BANKS = {0: 256, 256: 256, 512: 256, 768: 128, 896: 128}
 SCALAR_HEAD = {512: 104, 768: 96}
-CUT = 176
+CUT = 192
 
 
 def tile_picked_shuffle_mlp_none_perm_l_kernel(tc, xT, w1, w2, offs, out):
@@ -82,21 +82,25 @@ def tile_picked_shuffle_mlp_none_perm_l_kernel(tc, xT, w1, w2, offs, out):
             w2_first.append(sbuf([P, J, M], F32, "w2_first_%d" % m))
             nc.sync.dma_start(out=w2_first[m][:], in_=rows_of(w2, 0)[:, :, M * m : M * (m + 1)])
         nc.sync.dma_start(offsets[:], offs)
-        w2_left = sbuf([P, J, CUT], F32, "w2_left")
-        nc.sync.dma_start(out=w2_left[:], in_=rows_of(w2, 1)[:, :, :CUT])
-        w2_right = placed.tile([P, J, N - CUT], F32, name="w2_right", offset=0, align_bytes=256)
-        nc.sync.dma_start(out=w2_right[:], in_=rows_of(w2, 1)[:, :, CUT:])
+        w2_right = placed.tile([P, J, M], F32, name="w2_right", offset=512, align_bytes=256)
+        nc.sync.dma_start(out=w2_right[:], in_=rows_of(w2, 1)[:, :, M:])
+        w2_left = sbuf([P, J, M], F32, "w2_left")
+        nc.sync.dma_start(out=w2_left[:], in_=rows_of(w2, 1)[:, :, :M])
 
         identity = sbuf([P, P], F32, "identity")
         make_identity(nc, identity[:])
 
         w1_grouped = [sbuf([P, H, J], BF16, "w1_grouped_%d" % q) for q in range(2)]
         x_grouped = sbuf([P, 2 * T, J], BF16, "x_grouped")
-        window = sbuf([P, H], BF16, "window", on="w1_raw_1_%d" % SECOND_PASS[-2])
+        window = sbuf([P, H], F32, "window", on="w1_raw_1_%d" % SECOND_PASS[-2])
         h_banks = {c: psum.tile([P, n], F32, name="h_%d" % c, tag="bank_%d" % c) for c, n in BANKS.items()}
         w2_grouped = [sbuf([P, N, J], BF16, "w2_grouped_%d" % q) for q in range(2)]
         picked = [sbuf([P, KP], BF16, "picked_%d" % q) for q in range(2)]
-        h_grouped = [placed.tile([P, T * J], BF16, name="h_grouped_%d" % q, offset=2 * T * J * q, align_bytes=256) for q in range(2)]
+        token_parts = ((0, 0, T), (1, 0, T // 2), (1, T // 2, T))
+        h_grouped = {
+            (q, lo): placed.tile([P, (hi - lo) * J], BF16, name="h_grouped_%d_%d" % (q, lo), offset=2 * J * (T * q + lo), align_bytes=256)
+            for q, lo, hi in token_parts
+        }
         h_codes = sbuf([P, 2, T], U32, "h_codes")
         h_scales = [sbuf([P, T], U8, "h_scales_%d" % q) for q in range(2)]
 
@@ -157,31 +161,38 @@ def tile_picked_shuffle_mlp_none_perm_l_kernel(tc, xT, w1, w2, offs, out):
             codes, scales = quantise("w2_%d_%d" % (q, m), w2_grouped[q][:, M * m : M * (m + 1)], on)
             w2_mx[q, m] = (codes[:], scales[:])
 
-        def quantise_h(q):
-            nc.vector.quantize_mx(out=h_codes[:, q, :].bitcast(FP8X4), scales=h_scales[q][:], in_=h_grouped[q][:])
+        def quantise_h(q, lo, hi):
+            nc.vector.quantize_mx(out=h_codes[:, q, lo:hi].bitcast(FP8X4), scales=h_scales[q][:, lo:hi], in_=h_grouped[q, lo][:])
 
         interleave(on_vector, w2_grouped[0][:, :M], w2_first[0][:])
         quantise_w2(0, 0)
         interleave(on_vector, w2_grouped[0][:, M:], w2_first[1][:])
         for q in range(2):
-            nc.vector.tensor_copy(out=picked[q][:, :256], in_=window[:].indirect(offsets[:, 32 * q : 32 * q + 16]))
-            nc.scalar.activation(out=picked[q][:, 256:], in_=window[:].indirect(offsets[:, 32 * q + 16 : 32 * q + 32]), func=COPY)
-        interleave(on_scalar, w2_grouped[1][:, CUT:], w2_right[:])
+            dealt = picked[q][:].rearrange("p (u w e) -> p w u e", u=2, e=2)
+            nc.vector.tensor_copy(out=dealt[:, :64], in_=window[:].indirect(offsets[:, 32 * q : 32 * q + 16]))
+            nc.scalar.activation(out=dealt[:, 64:], in_=window[:].indirect(offsets[:, 32 * q + 16 : 32 * q + 32]), func=COPY)
+        interleave(on_scalar, w2_grouped[1][:, CUT:], w2_right[:, :, CUT - M :])
 
         for q in range(2):
             turned = psum.tile([P, 2, T], F32, name="turned_%d" % q, tag="turned_%d" % q)
             words = picked[q][:].bitcast(F32)
             for u in range(2):
-                nc.tensor.transpose(turned[:, u, :], words[:, u : KP // 2 : 2], identity[:])
-            on_scalar(h_grouped[q][:].bitcast(F32).rearrange("p (t u) -> p t u", u=2), turned[:].rearrange("p u t -> p t u"))
+                nc.tensor.transpose(turned[:, u, :], words[:, P * u : P * (u + 1)], identity[:])
+            for part, lo, hi in token_parts:
+                if part == q:
+                    on_scalar(h_grouped[q, lo][:].bitcast(F32).rearrange("p (t u) -> p t u", u=2), turned[:].rearrange("p u t -> p t u")[:, lo:hi])
 
-        for lo, hi in ((0, M), (M, CUT)):
-            interleave(on_vector, w2_grouped[1][:, lo:hi], w2_left[:, :, lo:hi])
+        interleave(on_vector, w2_grouped[1][:, M:CUT], w2_right[:, :, : CUT - M])
+        interleave(on_vector, w2_grouped[1][:, :M], w2_left[:])
+        held = placed.tile([P, M], U32, name="w2_held_codes", offset=2048, align_bytes=256)
+        held_scales = sbuf([P, M], U8, "w2_held_scales")
+        nc.vector.quantize_mx(out=held[:].bitcast(FP8X4), scales=held_scales[:], in_=w2_grouped[0][:, M:].rearrange("p c j -> p (c j)"))
+        w2_mx[0, 1] = (held[:], held_scales[:])
         quantise_w2(1, 0)
-        quantise_w2(0, 1, "w2_left")
-        quantise_h(0)
-        quantise_w2(1, 1, "picked_1")
-        quantise_h(1)
+        quantise_h(*token_parts[0])
+        quantise_w2(1, 1)
+        for part in token_parts[1:]:
+            quantise_h(*part)
 
         sums = [psum.tile([P, T], F32, name="sum_%d" % m, tag="bank_%d" % c) for m, c in enumerate((0, 256))]
         for q in range(2):

@@ -46,7 +46,7 @@ def tile_picked_shuffle_mlp_none_perm_l_kernel(tc, xT, w1, w2, offs, out):
             return w[q * KP : (q + 1) * KP, :].rearrange("(p j) c -> p j c", j=J)
 
         def interleave(copy, dst, src):
-            copy(dst.rearrange("p (b i) j -> p b j i", i=4), src.rearrange("p j (b i) -> p b j i", i=4))
+            copy(dst.rearrange("p (b i) j -> p b j i", i=2), src.rearrange("p j (b i) -> p b j i", i=2))
 
         def quantise(name, grouped, on=None):
             columns = grouped.shape[1]

from contextlib import ExitStack

import concourse.mybir as mybir
from concourse.masks import make_identity

K, T, H, N = 1024, 128, 1024, 256
FLOPS = 2 * K * H * T + 2 * H * N * T

F32 = mybir.dt.float32
BF16 = mybir.dt.bfloat16
U32 = mybir.dt.uint32
U16 = mybir.dt.uint16
U8 = mybir.dt.uint8
FP8X4 = mybir.dt.float8_e4m3fn_x4
COPY = mybir.ActivationFunctionType.Copy

P = 128
J = 4
KP = P * J
M = 128

FIRST_PASS = (0, 512)
SECOND_PASS = (0, 512, 768, 896)
BANKS = {0: 256, 256: 256, 512: 256, 768: 128, 896: 128}
SCALAR_HEAD = {512: 104, 768: 96}
CUT = 192


def tile_picked_shuffle_mlp_none_perm_l_kernel(tc, xT, w1, w2, offs, out):
    nc = tc.nc
    with ExitStack() as ctx:
        keep = ctx.enter_context(tc.tile_pool(name="keep", bufs=1))
        placed = ctx.enter_context(tc.tile_pool(name="placed", bufs=1))
        psum = ctx.enter_context(tc.psum_pool(name="psum", bufs=1))

        def sbuf(shape, dtype, name, on=None):
            return keep.tile(shape, dtype, name=name, tag=on or name, align_bytes=256)

        def on_vector(dst, src):
            nc.vector.tensor_copy(out=dst, in_=src)

        def on_scalar(dst, src):
            nc.scalar.copy(out=dst, in_=src)

        def rows_of(w, q):
            return w[q * KP : (q + 1) * KP, :].rearrange("(p j) c -> p j c", j=J)

        def interleave(copy, dst, src):
            copy(dst.rearrange("p (b i) j -> p b j i", i=2), src.rearrange("p j (b i) -> p b j i", i=2))

        def quantise(name, grouped, on=None):
            columns = grouped.shape[1]
            codes = sbuf([P, columns], U32, name + "_codes", on)
            scales = sbuf([P, columns], U8, name + "_scales")
            nc.vector.quantize_mx(out=codes[:].bitcast(FP8X4), scales=scales[:], in_=grouped.rearrange("p c j -> p (c j)"))
            return codes, scales

        def multiply(acc, stationary, moving, q):
            nc.tensor.matmul_mx(
                out=acc,
                lhsT=stationary[0].bitcast(FP8X4),
                lhsT_scale=stationary[1],
                rhs=moving[0].bitcast(FP8X4),
                rhs_scale=moving[1],
                start=(q == 0),
                stop=(q == 1),
            )

        offsets = keep.tile([P, H // 16], U16, name="offsets")
        x_raw = sbuf([P, 2, J, T], F32, "x_raw")
        nc.scalar.dma_start(
            out=x_raw[:].rearrange("p q j t -> p q (j t)"),
            in_=xT.rearrange("(q p j) t -> p q (j t)", q=2, j=J),
        )
        w1_raw = {}
        for q, starts in enumerate((FIRST_PASS, SECOND_PASS)):
            for lo, hi in zip(starts, starts[1:] + (H,)):
                w1_raw[q, lo] = sbuf([P, J, hi - lo], F32, "w1_raw_%d_%d" % (q, lo))
                nc.sync.dma_start(out=w1_raw[q, lo][:], in_=rows_of(w1, q)[:, :, lo:hi])
        w2_first = []
        for m in range(2):
            w2_first.append(sbuf([P, J, M], F32, "w2_first_%d" % m))
            nc.sync.dma_start(out=w2_first[m][:], in_=rows_of(w2, 0)[:, :, M * m : M * (m + 1)])
        nc.sync.dma_start(offsets[:], offs)
        w2_right = placed.tile([P, J, M], F32, name="w2_right", offset=512, align_bytes=256)
        nc.sync.dma_start(out=w2_right[:], in_=rows_of(w2, 1)[:, :, M:])
        w2_left = sbuf([P, J, M], F32, "w2_left")
        nc.sync.dma_start(out=w2_left[:], in_=rows_of(w2, 1)[:, :, :M])

        identity = sbuf([P, P], F32, "identity")
        make_identity(nc, identity[:])

        w1_grouped = [sbuf([P, H, J], BF16, "w1_grouped_%d" % q) for q in range(2)]
        x_grouped = sbuf([P, 2 * T, J], BF16, "x_grouped")
        window = sbuf([P, H], F32, "window", on="w1_raw_1_%d" % SECOND_PASS[-2])
        h_banks = {c: psum.tile([P, n], F32, name="h_%d" % c, tag="bank_%d" % c) for c, n in BANKS.items()}
        w2_grouped = [sbuf([P, N, J], BF16, "w2_grouped_%d" % q) for q in range(2)]
        picked = [sbuf([P, KP], BF16, "picked_%d" % q) for q in range(2)]
        token_parts = ((0, 0, T), (1, 0, T // 2), (1, T // 2, T))
        h_grouped = {
            (q, lo): placed.tile([P, (hi - lo) * J], BF16, name="h_grouped_%d_%d" % (q, lo), offset=2 * J * (T * q + lo), align_bytes=256)
            for q, lo, hi in token_parts
        }
        h_codes = sbuf([P, 2, T], U32, "h_codes")
        h_scales = [sbuf([P, T], U8, "h_scales_%d" % q) for q in range(2)]

        x_mx = {}
        w1_mx = {}

        def interleave_w1(copy, q, piece, lo, hi):
            interleave(copy, w1_grouped[q][:, lo:hi, :], w1_raw[q, piece][:, :, lo - piece : hi - piece])

        def quantise_x(q, on=None):
            codes, scales = quantise("x_%d" % q, x_grouped[:, q * T : (q + 1) * T, :], on)
            x_mx[q] = (codes[:], scales[:])

        def quantise_w1(q, lo, hi):
            codes, scales = quantise("w1_%d_%d" % (q, lo), w1_grouped[q][:, lo:hi])
            for c, n in BANKS.items():
                if lo <= c < hi:
                    w1_mx[q, c] = (codes[:, c - lo : c - lo + n], scales[:, c - lo : c - lo + n])

        def close_bank(c):
            quantise_w1(1, c, c + BANKS[c])
            multiply(h_banks[c][:], x_mx[1], w1_mx[1, c], 1)

        for q, copy in enumerate((on_vector, on_scalar)):
            interleave(copy, x_grouped[:, q * T : (q + 1) * T, :], x_raw[:, q])
        quantise_x(1)
        for piece in FIRST_PASS:
            interleave_w1(on_scalar, 0, piece, piece + 256, piece + 512)
            interleave_w1(on_vector, 0, piece, piece, piece + 256)
            quantise_w1(0, piece, piece + 256)
            quantise_w1(0, piece + 256, piece + 512)
        quantise_x(0, on="w1_grouped_0")
        for c in BANKS:
            multiply(h_banks[c][:], x_mx[0], w1_mx[0, c], 0)

        interleave_w1(on_scalar, 1, 0, 256, 512)
        interleave_w1(on_vector, 1, 0, 0, 256)
        close_bank(0)
        for piece, behind in ((512, 256), (768, 512)):
            head = piece + SCALAR_HEAD[piece]
            interleave_w1(on_scalar, 1, piece, piece, head)
            interleave_w1(on_vector, 1, piece, head, piece + BANKS[piece])
            close_bank(behind)
        interleave_w1(on_vector, 1, 896, 896, 960)
        interleave_w1(on_scalar, 1, 896, 960, H)
        close_bank(768)
        codes = sbuf([P, 128], U32, "w1_last_codes")
        scales = sbuf([P, 128], U8, "w1_last_scales")
        for lo in (0, 64):
            nc.vector.quantize_mx(out=codes[:, lo : lo + 64].bitcast(FP8X4), scales=scales[:, lo : lo + 64], in_=w1_grouped[1][:, 896 + lo : 960 + lo].rearrange("p c j -> p (c j)"))
        multiply(h_banks[896][:], x_mx[1], (codes[:], scales[:]), 1)
        for c, n in BANKS.items():
            on_scalar(window[:, c : c + n], h_banks[c][:])

        w2_mx = {}

        def quantise_w2(q, m, on=None):
            codes, scales = quantise("w2_%d_%d" % (q, m), w2_grouped[q][:, M * m : M * (m + 1)], on)
            w2_mx[q, m] = (codes[:], scales[:])

        def quantise_h(q, lo, hi):
            nc.vector.quantize_mx(out=h_codes[:, q, lo:hi].bitcast(FP8X4), scales=h_scales[q][:, lo:hi], in_=h_grouped[q, lo][:])

        interleave(on_vector, w2_grouped[0][:, :M], w2_first[0][:])
        quantise_w2(0, 0)
        interleave(on_vector, w2_grouped[0][:, M:], w2_first[1][:])
        for q in range(2):
            dealt = picked[q][:].rearrange("p (u w e) -> p w u e", u=2, e=2)
            nc.vector.tensor_copy(out=dealt[:, :64], in_=window[:].indirect(offsets[:, 32 * q : 32 * q + 16]))
            nc.scalar.activation(out=dealt[:, 64:], in_=window[:].indirect(offsets[:, 32 * q + 16 : 32 * q + 32]), func=COPY)
        interleave(on_scalar, w2_grouped[1][:, CUT:], w2_right[:, :, CUT - M :])

        for q in range(2):
            turned = psum.tile([P, 2, T], F32, name="turned_%d" % q, tag="turned_%d" % q)
            words = picked[q][:].bitcast(F32)
            for u in range(2):
                nc.tensor.transpose(turned[:, u, :], words[:, P * u : P * (u + 1)], identity[:])
            for part, lo, hi in token_parts:
                if part == q:
                    on_scalar(h_grouped[q, lo][:].bitcast(F32).rearrange("p (t u) -> p t u", u=2), turned[:].rearrange("p u t -> p t u")[:, lo:hi])

        interleave(on_vector, w2_grouped[1][:, M:CUT], w2_right[:, :, : CUT - M])
        interleave(on_vector, w2_grouped[1][:, :M], w2_left[:])
        held = placed.tile([P, M], U32, name="w2_held_codes", offset=2048, align_bytes=256)
        held_scales = sbuf([P, M], U8, "w2_held_scales")
        nc.vector.quantize_mx(out=held[:].bitcast(FP8X4), scales=held_scales[:], in_=w2_grouped[0][:, M:].rearrange("p c j -> p (c j)"))
        w2_mx[0, 1] = (held[:], held_scales[:])
        quantise_w2(1, 0)
        quantise_h(*token_parts[0])
        quantise_w2(1, 1)
        for part in token_parts[1:]:
            quantise_h(*part)

        sums = [psum.tile([P, T], F32, name="sum_%d" % m, tag="bank_%d" % c) for m, c in enumerate((0, 256))]
        for q in range(2):
            for m in range(2):
                multiply(sums[m][:], w2_mx[q, m], (h_codes[:, q, :], h_scales[q][:]), q)
        result = sbuf([P, 2, T], F32, "result")
        on_vector(result[:, 0, :], sums[0][:])
        on_scalar(result[:, 1, :], sums[1][:])
        nc.sync.dma_start(out=out.rearrange("(m p) t -> p m t", m=2), in_=result[:])
